import numpy as np, ml_dtypes
CORES = [113,118,241,246]
N = 4
BF = ml_dtypes.bfloat16
def gentries(a):
    return np.ascontiguousarray(a.reshape(8, 16, -1).transpose(0, 2, 1)).reshape(8, -1)
def gtable(e):
    e = np.asarray(e); return np.ascontiguousarray(e.reshape(8, -1, 16).transpose(0, 2, 1)).reshape(128, -1).astype(np.int32)
S, R, B, C, P, STEPS, O = 1568, 1568, 160, 3, 3, 2, 480
def pick(t, l):
    return np.stack([np.stack([np.take(t[r, g], l[r, g], axis=1) for g in range(8)]) for r in range(N)])
def widen(t, send):
    s = pick(t, send)
    return np.stack([np.concatenate([t[r]] + [s[(r + 1 + m) % N][:, :, (N - 2 - m) * B:(N - 1 - m) * B] for m in range(N - 1)], axis=2) for r in range(N)])
def groups(a):
    return np.stack([gentries(v) for v in a])
def first(v):
    u, i, n = np.unique(v, return_index=True, return_inverse=True); return i[n.reshape(-1)]
def network(rng, pairs):
    reac = np.zeros((N, 8, 2 * R), np.int64); cons = np.full((N, 8, C * S), R + O); sp = np.zeros((N, 8, O), np.int64); rx = np.zeros((N, 8, O), np.int64)
    for g in range(8):
        inc, use = [], []
        for r in range(N):
            if pairs:
                inc.append((rng.permutation(R)[:, None] + R * np.arange(2)).reshape(-1)); use.append((rng.permutation(S)[:, None] + S * np.arange(C)).reshape(-1)[:2 * R])
            else:
                inc.append(rng.permutation(2 * R)); use.append(rng.permutation(C * S)[:2 * R])
            e, u = inc[r], use[r]
            rx[r, g] = e[:O] % R; sp[r, g] = u[:O] % S
            reac[r, g, e[O:]] = u[O:] % S; cons[r, g, u[O:]] = e[O:] % R
        for r in range(N):
            for m in range(N - 1):
                q, k = (r + 1 + m) % N, N - 2 - m
                e = inc[r][m * B:(m + 1) * B]; u = use[q][k * B:(k + 1) * B]; n = np.arange(B); j = n if pairs else rng.permutation(B)
                reac[r, g, e] = S + m * B + (first(u % S) if pairs else j)
                cons[q, g, u[j]] = R + k * B + (first(e % R) if pairs else n)
    prod = rng.integers(0, R + O, (N, 8, P * S)); prod[rng.random(prod.shape) < 0.25] = R + O
    return reac, cons, prod, sp, rx
def pack(x, rate, net):
    return dict([("x", np.ascontiguousarray(np.reshape(x, (N, 128, S))).astype(np.int32)), ("rate", rate.astype(np.int32))] + [(n, np.stack([gtable(e) for e in v])) for n, v in zip(("reac", "cons", "prod", "spsend", "rxsend"), net)])
def some(rng):
    return rng.integers(0, 256, (N, 8, 16, S)) >> rng.integers(0, 8, (N, 8, 16, S)), rng.integers(1, 128, (N, 8, R)) >> rng.integers(0, 4, (N, 8, R))
def setup_inputs(rng):
    net = network(rng, False); x, k = some(rng); return pack(x, k, net)
def setup_inputs_ties(rng):
    net = network(rng, False); n = np.sum(net[1].reshape(N, 8, C, S) != R + O, axis=2)[:, :, None]
    x = np.where(n < 2, 5 + rng.integers(0, 4, (N, 8, 16, S)), 3 * n - rng.integers(0, 2, (N, 8, 16, S)))
    return pack(x, rng.integers(123, 128, (N, 8, R)), net)
def setup_inputs_twins(rng):
    net = network(rng, True); x, k = some(rng); return pack(x, k, net)
def setup_inputs_ends(rng):
    net = network(rng, False); p = rng.choice(np.array([0, R - 1, R, R + O - 1, R + O]), (N, 8, P * S))
    x = 255 * (rng.random((N, 8, 16, S)) < 0.9); k = 127 * (rng.random((N, 8, R)) < 0.9)
    return pack(x, k, net[:2] + (p,) + net[3:])
def setup_inputs_spread(rng):
    net = network(rng, False); w = rng.random((N, 8, 1, S)); x = rng.integers(0, 256, (N, 8, 16, S))
    x = np.where(w < 0.05, 0, np.where(w < 0.15, 255, np.where(w < 0.5, x, x >> 5)))
    w = rng.random((N, 8, R)); k = rng.integers(0, 128, (N, 8, R)); k = np.where(w < 0.05, 0, np.where(w < 0.15, 127, np.where(w < 0.5, k, k >> 4)))
    return pack(x, k, net)
def check_inputs(d):
    try:
        top = {"x": 255, "rate": 127, "reac": S + O - 1, "cons": R + O, "prod": R + O, "spsend": S - 1, "rxsend": R - 1}
        bad = [n + " range" for n in top if d[n].min() < 0 or d[n].max() > top[n]]
        if bad: return bad
        ra, co, ss, rs = groups(d["reac"]), groups(d["cons"]), groups(d["spsend"]), groups(d["rxsend"])
        ids = np.broadcast_to(np.arange(N * S, dtype=np.int64).reshape(N, 1, 1, S), (N, 8, 1, S)); idr = np.broadcast_to(np.arange(N * R, dtype=np.int64).reshape(N, 1, 1, R), (N, 8, 1, R))
        net = np.arange(8, dtype=np.int64).reshape(1, 8, 1); own = np.arange(N, dtype=np.int64).reshape(N, 1, 1)
        a = (net * (N * S) + pick(widen(ids, ss), ra)[:, :, 0]) * (N * R) + own * R + np.arange(2 * R) % R
        w = pick(np.concatenate([widen(idr, rs), np.full((N, 8, 1, 1), -1)], axis=3), co)[:, :, 0]
        b = ((net * (N * S) + own * S + np.arange(C * S) % S) * (N * R) + w)[w >= 0]
        return [] if np.array_equal(np.sort(a.reshape(-1)), np.sort(b)) else ["cons fits reac"]
    except Exception:
        return ["form"]
def reference(x, rate, reac, cons, prod, spsend, rxsend):
    n = x.astype(np.int32).reshape(N, 8, 16, S); k = rate.astype(np.int32)[:, :, None]; none = np.zeros((N, 8, 16, 1), np.int32)
    ra, co, pr, ss, rs = groups(reac), groups(cons), groups(prod), groups(spsend), groups(rxsend)
    for step in range(STEPS):
        a = pick(widen(n, ss), ra)
        f = np.minimum(3, (k * a[..., :R] * a[..., R:]) >> 10)
        w = np.concatenate([widen(f, rs), none], axis=3)
        demand = np.sum(pick(w, co).reshape(N, 8, 16, C, S), axis=3)
        veto = (demand > n).astype(np.int32)
        b = pick(widen(veto, ss), ra)
        f = f * ((b[..., :R] + b[..., R:]) == 0)
        w = np.concatenate([widen(f, rs), none], axis=3)
        n = n - np.sum(pick(w, co).reshape(N, 8, 16, C, S), axis=3) + np.sum(pick(w, pr).reshape(N, 8, 16, P, S), axis=3)
    return {"y": n.reshape(N, 128, S).astype(np.float32)}

@@ -1,0 +1,391 @@
+from concourse.bass import DstId, RemoteDMATransfer
+from concourse.mybir import AluOpType, ActivationFunctionType
+
+S = 1568
+AC = [(0, 480), (480, 576), (1056, 512)]
+CO = [(0, 992), (992, 576)]
+HALF = 128.500244140625
+LW = CO[1][1] // 4
+
+SCRATCH = {
+    "sx": ("dram", [4, 128, 392], "bfloat16"), "lx": ("dram", [4, 128, 392], "bfloat16"),
+    "se": ("dram", [4, 128, 98], "int32"), "le": ("dram", [4, 128, 98], "int32"),
+    "sl": ("dram", [4, 128, 147], "int32"), "ll": ("dram", [4, 128, 147], "int32"),
+    "E32": ("sbuf", [128, 392], "int32"), "LST": ("sbuf", [128, 392], "uint16"), "CPL": ("sbuf", [128, 588], "uint16"),
+    "IW": ("sbuf", [128, 256], "int32"), "IM": ("sbuf", [128, 16], "int32"), "IB": ("sbuf", [128, 128], "int32"),
+    "JW": ("sbuf", [128, 256], "int32"), "JM": ("sbuf", [128, 16], "int32"), "JB": ("sbuf", [128, 128], "int32"),
+    "W": ("sbuf", [128, 256], "bfloat16"), "NI": ("sbuf", [128, 128], "bfloat16"), "I4": ("sbuf", [128, 128], "bfloat16"),
+    "BO": ("sbuf", [128, 128], "bfloat16"), "MK": ("sbuf", [128, 16], "float32"), "BK": ("sbuf", [128, 2048], "bfloat16"),
+    "RB": ("sbuf", [128, 98], "bfloat16"), "K": ("sbuf", [128, S], "float32"),
+    "N0": ("sbuf", [128, 2048], "bfloat16"), "N1": ("sbuf", [128, 2048], "float32"), "ON": ("sbuf", [128, S], "float16"),
+    "LY": ("sbuf", [128, 3 * LW], "float16"), "LF": ("sbuf", [128, 3 * LW], "float32"),
+    "pa": ("psum", [128, 1024], "float32"), "pb": ("psum", [128, 1024], "float32"), "pk": ("psum", [128, 512], "float32"),
+    "pe0": ("psum", [128, 512], "float32"), "pe1": ("psum", [128, 512], "float32"), "pe2": ("psum", [128, 512], "float32"),
+    "so0": ("dram", [4, 128, CO[0][1] // 4], "float16"), "ly0": ("dram", [4, 128, CO[0][1] // 4], "float16"),
+    "so1": ("dram", [4, 128, LW], "float16"),
+}
+for _s in range(2):
+    for _n, _w, _d in (("SE0", 480, "bfloat16"), ("SE1", 480, "bfloat16"), ("SE2", 480, "bfloat16"), ("SE3", 480, "bfloat16"),
+                       ("X1", 480, "bfloat16"), ("X2", 480, "bfloat16"),
+                       ("TA", S, "float32"), ("TP", S, "float32"), ("FA", S, "bfloat16"), ("FB", S, "bfloat16"),
+                       ("FW", 2064, "bfloat16"), ("UW", 2048, "bfloat16"), ("GW", 2064, "bfloat16"),
+                       ("DG", 3 * S, "bfloat16"), ("DB", S, "float32"), ("VT", S, "bfloat16"), ("VG", 2 * S, "bfloat16"),
+                       ("UG", 6 * S, "bfloat16"), ("UA", S, "float32")):
+        SCRATCH["%s_%d" % (_n, _s)] = ("sbuf", [128, _w], _d)
+
+SEMAPHORES = (["cv", "cs", "ct", "cg", "rl", "se", "sl", "gx", "gl", "gy", "yy", "EE", "XX", "o0", "o1", "ay0", "ay1"]
+              + ["%s%d" % (a, r) for a in ("ae", "ax", "al") for r in range(4)])
+
+
+def masks(src, cores, topo):
+    others = [c for c in cores if c != src]
+    eng = dict((c, list(topo.engines(src, c))) for c in others)
+    few = min(len(eng[c]) for c in others)
+    far = [c for c in others if len(eng[c]) == few]
+    share = len(eng[far[0]]) // len(far)
+    share = 1 << (share.bit_length() - 1)
+    out = {}
+    for i, c in enumerate(far):
+        out[c] = eng[c][i * share:(i + 1) * share]
+    for c in others:
+        if c not in out:
+            out[c] = [e for e in eng[c] if e not in eng[far[0]]][0:4:2]
+    return out
+
+
+def rank_program(g, core, T, topo):
+    me = T.rank_of(core)
+    if me is None:
+        return
+    add, sub, mult, amin = AluOpType.add, AluOpType.subtract, AluOpType.mult, AluOpType.min
+    eq, le = AluOpType.is_equal, AluOpType.is_le
+    act = ActivationFunctionType
+    cores = list(T.cores)
+    N = len(cores)
+    others = [r for r in range(N) if r != me]
+    near = [r for r in others if cores[r] in topo.cores_of(core)]
+    order = near + [r for r in others if r not in near]
+    eng = masks(core, cores, topo)
+    inc = dict((r, len(masks(cores[r], cores, topo)[core])) for r in others)
+
+    queue = {"v": g.vector, "s": g.scalar, "t": g.tensor, "g": g, "y": g.sync}
+    total, waited, hist = {}, {}, {}
+    know = dict((k, {}) for k in queue)
+
+    def wait(k, toks):
+        best = {}
+        for sem, val, clock in toks:
+            if know[k].get(sem, 0) < val and (sem not in best or best[sem][1] < val):
+                best[sem] = (sem, val, clock)
+        todo = [t for t in best.values() if not any(u[0] != t[0] and u[2].get(t[0], 0) >= t[1] for u in best.values())]
+        for sem, val, clock in todo:
+            queue[k].wait_ge(T.sem[sem], val)
+            waited[sem] = max(waited.get(sem, 0), val)
+            for s, v in list(clock.items()) + [(sem, val)]:
+                know[k][s] = max(know[k].get(s, 0), v)
+
+    def hazards(k, rd, wr):
+        toks = []
+        for kind, regs in ((0, rd), (1, wr)):
+            for b, lo, hi, p0, p1 in regs:
+                bank = b[0] == "p"
+                for lo2, hi2, q0, q1, w2, tok, k2 in hist.get(b, []):
+                    if bank and k2 != k:
+                        hit = lo // 512 <= (hi2 - 1) // 512 and lo2 // 512 <= (hi - 1) // 512
+                    elif bank:
+                        hit = False
+                    else:
+                        hit = lo < hi2 and lo2 < hi and p0 < q1 and q0 < p1 and (kind or w2)
+                    if hit:
+                        toks.append(tok)
+        return toks
+
+    def note(k, rd, wr, tok):
+        for w, regs in ((0, rd), (1, wr)):
+            for b, lo, hi, p0, p1 in regs:
+                hist.setdefault(b, []).append((lo, hi, p0, p1, w, tok, k))
+
+    def reg(b, lo, hi, p0=0, p1=128):
+        return (b, lo, hi, p0, p1)
+
+    def op(k, rd, wr, call):
+        wait(k, hazards(k, rd, wr))
+        sem = "c" + k
+        total[sem] = total.get(sem, 0) + 1
+        clock = dict(know[k])
+        clock[sem] = total[sem]
+        note(k, rd, wr, (sem, total[sem], clock))
+        call().then_inc(T.sem[sem], 1)
+
+    def dma(k, out, in_, sem, full, rd, wr):
+        wait(k, hazards(k, rd, wr))
+        total[sem] = total.get(sem, 0) + 16
+        note(k, rd, wr, (sem, full, dict(know[k]) if full == 16 else {}))
+        queue[k].dma_start(out, in_).then_inc(T.sem[sem], 16)
+
+    def send(src, dst, sems, rd):
+        wait("g", hazards("g", rd, []))
+        trs = []
+        for r in order:
+            rid, pid = topo.addr(cores[r], core)
+            m = 0
+            for e in eng[cores[r]]:
+                m |= 1 << e
+            trs.append(RemoteDMATransfer(dst_ids=[DstId(rid=rid, pnc=pid)], dma_engine_mask=m, remote_sem=T.sem[sems],
+                                         src=T[src][r], dst=dst(r)))
+            total["rl"] = total.get("rl", 0) + len(eng[cores[r]])
+        g.remote_dma_fused(trs, local_sem=T.sem["rl"])
+
+    def arrives(sem, regs, srcs):
+        n = sum(inc[r] for r in srcs)
+        total[sem] = total.get(sem, 0) + n
+        note("r", [], regs, (sem, n, {}))
+
+    def ap(x):
+        return T[x[0]][:, x[1]:x[2]]
+
+    def ind(win, wn, lst, c0, n):
+        return T[win][:, 0:wn].indirect(T[lst][:, c0:c0 + n // 16])
+
+    def pick(k, out, win, wn, lst, c0):
+        n = out[2] - out[1]
+        rd = [reg(win, 0, wn), reg(lst, c0, c0 + n // 16)]
+        if k == "v":
+            op("v", rd, [reg(*out)], lambda: g.vector.tensor_copy(out=ap(out), in_=ind(win, wn, lst, c0, n)))
+        else:
+            op("s", rd, [reg(*out)], lambda: g.scalar.activation(out=ap(out), in_=ind(win, wn, lst, c0, n), func=act.Copy))
+
+    def pickop(out, win, wn, lst, c0, other, o):
+        n = out[2] - out[1]
+        op("v", [reg(win, 0, wn), reg(lst, c0, c0 + n // 16), reg(*other)], [reg(*out)],
+           lambda: g.vector.tensor_tensor(out=ap(out), in0=ind(win, wn, lst, c0, n), in1=ap(other), op=o))
+
+    def tt(out, a, b, o):
+        op("v", [reg(*a), reg(*b)], [reg(*out)], lambda: g.vector.tensor_tensor(out=ap(out), in0=ap(a), in1=ap(b), op=o))
+
+    def ts(out, a, s1, o1, s2=None, o2=None, more=()):
+        if o2 is None:
+            f = lambda: g.vector.tensor_scalar(out=ap(out), in0=ap(a), scalar1=s1, scalar2=None, op0=o1)
+        else:
+            f = lambda: g.vector.tensor_scalar(out=ap(out), in0=ap(a), scalar1=s1, scalar2=s2, op0=o1, op1=o2)
+        op("v", [reg(*a)] + list(more), [reg(*out)], f)
+
+    def actv(out, a, func, bias=0.0, scale=1.0, more=()):
+        if func == act.Copy:
+            f = lambda: g.scalar.activation(out=ap(out), in_=ap(a), func=func)
+        else:
+            f = lambda: g.scalar.activation(out=ap(out), in_=ap(a), func=func, bias=bias, scale=scale)
+        op("s", [reg(*a)] + list(more), [reg(*out)], f)
+
+    def copy(k, out, a):
+        if k == "v":
+            op("v", [reg(*a)], [reg(*out)], lambda: g.vector.tensor_copy(out=ap(out), in_=ap(a)))
+        else:
+            actv(out, a, act.Copy)
+
+    def mm(out, lhs, rhs, start, stop):
+        op("t", [reg(*lhs), reg(*rhs)], [reg(*out)],
+           lambda: g.tensor.matmul(out=ap(out), lhsT=ap(lhs), rhs=ap(rhs), start=start, stop=stop))
+
+    def mmw(pb, p0, lhs, rb, r0, n, start, stop):
+        for c in range(0, n, 512):
+            m = min(512, n - c)
+            mm((pb, p0 + c, p0 + c + m), lhs, (rb, r0 + c, r0 + c + m), start, stop)
+
+    EYE, NEG, I4 = ("W", 0, 128), ("NI", 0, 128), ("I4", 0, 128)
+
+    dma("g", T.sx[:], T.x[:], "gx", 16, [], [reg("sx", 0, 4)])
+    for k, j, a, b, t in (("y", 0, 0, 98, T.reac[:, 0:98]), ("s", 3, 0, 30, T.spsend[:]), ("y", 1, 0, 98, T.reac[:, 98:196]),
+                          ("s", 3, 30, 60, T.rxsend[:]), ("y", 2, 0, 98, T.rate[:]),
+                          ("s", 3, 60, 98, T.reac[:, 0:38])):
+        dma(k, T.se[:, j::4, a:b], t, "se", 96, [], [reg("se", 0, 4, 30 * j + a // 30, 30 * j + a // 30 + 1)])
+    for j in range(2):
+        dma("s", T.sl[:, j::4, :], T.cons[:, 147 * j:147 * j + 147], "sl", 64, [], [reg("sl", 0, 4, j, j + 1)])
+        dma("y", T.sl[:, 2 + j::4, :], T.prod[:, 147 * j:147 * j + 147], "sl", 64, [], [reg("sl", 0, 4, 2 + j, 3 + j)])
+
+    op("g", [], [reg("IB", 0, 128)], lambda: g.iota(T.IB[:], [[-16, 8], [0, 16]], 128, 1))
+    op("g", [], [reg("IM", 0, 16)], lambda: g.iota(T.IM[:], [[-1, 16]], 128, 1))
+    op("g", [], [reg("IW", 0, 256)], lambda: g.iota(T.IW[:], [[-1, 256]], 256, 1))
+    for a, b, c in (("se", "le", "ae"), ("sx", "lx", "ax"), ("sl", "ll", "al")):
+        send(a, lambda r: T[b][me], "%s%d" % (c, me), [reg(a, 0, 4)])
+        for r in others:
+            arrives("%s%d" % (c, r), [reg(b, r, r + 1)], [r])
+
+    for b in ("FW_0", "GW_0", "FW_1", "GW_1"):
+        op("v", [], [reg(b, 2048, 2064)], lambda: g.vector.memset(T[b][:, 2048:2064], 0.0))
+    ts(("JB", 0, 128), ("IB", 0, 128), 4, AluOpType.arith_shift_right)
+    ts(("JM", 0, 16), ("IM", 0, 16), 15, AluOpType.bitwise_and)
+    ts(("BO", 0, 128), ("JB", 0, 128), 8, eq)
+    ts(("MK", 0, 16), ("JM", 0, 16), 0, eq, 1.0 / 1024, mult)
+    for c in range(16):
+        o, m = ("BK", 128 * c, 128 * c + 128), reg("MK", c, c + 1)
+        if c % 2:
+            actv(o, ("BO", 0, 128), act.Identity, 0.0, T.MK[:, c:c + 1], [m])
+        else:
+            ts(o, ("BO", 0, 128), T.MK[:, c:c + 1], mult, None, None, [m])
+    ts(("JW", 0, 256), ("IW", 0, 256), 127, AluOpType.bitwise_and)
+    ts(("W", 0, 256), ("JW", 0, 256), 0, eq)
+    ts(("NI", 0, 128), ("JW", 0, 128), 0, eq, -1, mult)
+    ts(("I4", 0, 128), ("JW", 0, 128), 0, eq, 4, mult)
+
+    for sem, a, b, buf, n in (("EE", "se", "le", "E32", 392), ("XX", "sx", "lx", "N0", S)):
+        for r in [me] + order:
+            t = a if r == me else b
+            dma("y", T[buf][32 * r:32 * r + 32, 0:n], T[t][r], sem, 64, [reg(t, r, r + 1)], [reg(buf, 0, n, 32 * r, 32 * r + 32)])
+    for r in [me] + order:
+        t = "sl" if r == me else "ll"
+        dma("g", T.CPL[32 * r:32 * r + 32, :], T[t][r], "gl", 64, [reg(t, r, r + 1)], [reg("CPL", 0, 588, 32 * r, 32 * r + 32)])
+    copy("v", ("RB", 0, 98), ("E32", 196, 294))
+    copy("v", ("LST", 0, 354), ("E32", 0, 354))
+
+    def spread(p, p0, c0, c1):
+        for c in range(c0, c1):
+            a = p0 + 98 * (c - c0)
+            mm((p, a, a + 98), ("BK", 128 * c, 128 * c + 128), ("RB", 0, 98), True, True)
+    for k, p, p0, c0, c1 in (("s", "pa", 0, 4, 9), ("v", "pa", 512, 9, 13), ("s", "pb", 0, 13, 16)):
+        spread(p, p0, c0, c1)
+        copy(k, ("K", 98 * c0, 98 * c1), (p, p0, p0 + 98 * (c1 - c0)))
+
+    RE, SP, RXL = 0, 294, 324
+
+    def border(s, e, win, c0):
+        se = "SE%d_%d" % (e, s)
+        pick("v", (se, 224, 480), win, S, "LST", c0 + 14)
+        pick("s", (se, 0, 224), win, S, "LST", c0)
+        for m, k in ((2, "s"), (0, "v"), (1, "s")):
+            mm(("pe%d" % m, 0, 160), ("W", 32 * (1 + m), 32 * (1 + m) + 128), (se, 160 * (2 - m), 160 * (3 - m)), True, True)
+            copy(k, (win, S + 160 * m, S + 160 * m + 160), ("pe%d" % m, 0, 160))
+
+    for s in range(2):
+        def nm(b):
+            return "%s_%d" % (b, s)
+        NW, FW, UW, GW = "N%d" % s, nm("FW"), nm("UW"), nm("GW")
+        border(s, 0, NW, SP)
+        if s == 0:
+            spread("pk", 0, 0, 5)
+
+        def kx(i, h):
+            a, n = AC[i]
+            o, x = ((nm("TA"), a, a + n), ("K", a, a + n)) if h == 0 else ((nm("TP"), a, a + n), (nm("TA"), a, a + n))
+            pickop(o, NW, 2048, "LST", RE + 98 * h + a // 16, x, mult)
+
+        def whole(i, k):
+            a, n = AC[i]
+            p, fa, fb, f = [(b, a, a + n) for b in (nm("TP"), nm("FA"), nm("FB"), FW)]
+            if k == "s":
+                actv(fa, p, act.Identity, HALF, 1.0)
+                actv(fb, fa, act.Relu, 132.0, -1.0)
+                actv(f, fb, act.Identity, 3.0, -1.0)
+            else:
+                ts(fa, p, 3.4, amin, HALF, add)
+                ts(f, fa, -129.0, add)
+        n = AC[0][1]
+        pick("s", (nm("X2"), 0, n), NW, 2048, "LST", RE + 98)
+        mm(("pa", 0, n), EYE, (nm("X2"), 0, n), True, True)
+        pick("s", (nm("X1"), 0, n), NW, 2048, "LST", RE)
+        kx(1, 0)
+        kx(1, 1)
+        whole(1, "s")
+        tt((nm("TA"), 0, n), ("pa", 0, n), (nm("X1"), 0, n), mult)
+        tt((nm("TP"), 0, n), ("pk", 0, n), (nm("TA"), 0, n), mult)
+        whole(0, "s")
+        kx(2, 0)
+        kx(2, 1)
+        whole(2, "v")
+        border(s, 1, FW, RXL)
+        DB, DG = nm("DB"), nm("DG")
+        A = 896
+        D = [(0, 608, "pa"), (608, A - 608, "pb")]
+        for a, n, p in D:
+            for c in range(3):
+                pick("s", (DG, S * c + a, S * c + a + n), FW, 2049, "CPL", 98 * c + a // 16)
+                mmw(p, 0, EYE, DG, S * c + a, n, c == 0, c == 2)
+        for c in range(3):
+            pickop((DB, A, S), FW, 2049, "CPL", 98 * c + A // 16, (NW if c == 0 else DB, A, S), sub if c == 0 else add)
+        ts((UW, A, S), (DB, A, S), 0.0, le)
+        for a, n, p in D:
+            tt((UW, a, a + n), (p, 0, n), (NW, a, a + n), le)
+        border(s, 2, UW, SP)
+        VT, VG = nm("VT"), nm("VG")
+        A = 960
+        mmw("pb", 0, EYE, FW, A, S - A, True, False)
+        pick("s", (VG, A, S), UW, 2048, "LST", RE + A // 16)
+        mmw("pb", 0, I4, VG, A, S - A, False, False)
+        for a, n in ((A, 512), (A + 512, S - A - 512)):
+            pick("s", (VG, S + a, S + a + n), UW, 2048, "LST", RE + 98 + a // 16)
+            mmw("pb", a - A, I4, VG, S + a, n, False, True)
+        for h in range(2):
+            pickop((VT, 0, A) if h == 0 else (GW, 0, A), UW, 2048, "LST", RE + 98 * h, (FW, 0, A) if h == 0 else (VT, 0, A), mult)
+        for a, n in ((A, 512), (A + 512, S - A - 512)):
+            actv((GW, a, a + n), ("pb", a - A, a - A + n), act.Relu, -8.0, 1.0)
+        border(s, 3, GW, RXL)
+        UA, UG = nm("UA"), nm("UG")
+        out = "N1" if s == 0 else "ON"
+
+        def uv(a, n, j):
+            acc = (UA, a, a + n)
+            pickop((out, a, a + n) if j == 5 else acc, GW, 2049, "CPL", 98 * j + a // 16,
+                   (NW, a, a + n) if j == 0 else acc, sub if j in (0, 3) else add)
+
+        def us(a, n, j, p0):
+            pick("s", (UG, S * j + a, S * j + a + n), GW, 2049, "CPL", 98 * j + a // 16)
+            mmw("pa", p0, NEG if j < 3 else EYE, UG, S * j + a, n, j == 0, j == 5)
+
+        def fin(a, n, p0):
+            tt((out, a, a + n), ("pa", p0, p0 + n), (NW, a, a + n), add)
+
+        def ship(i):
+            a, n = CO[i]
+            dma("y", T["so%d" % i][:], T.ON[:, a:a + n], "o%d" % i, 16, [reg("ON", a, a + n)], [reg("so%d" % i, 0, 4)])
+        if s == 0:
+            for j in range(5):
+                us(0, 800, j, 0)
+            us(0, 512, 5, 0)
+            us(512, 288, 5, 512)
+            for j in range(6):
+                uv(800, 768, j)
+            fin(0, 512, 0)
+            fin(512, 288, 512)
+        else:
+            for j in range(6):
+                us(0, 512, j, 0)
+            for j in range(6):
+                us(992, 288, j, 512)
+            for j in range(6):
+                uv(512, 480, j)
+            uv(1280, 288, 0)
+            fin(0, 512, 0)
+            ship(0)
+            for j in range(1, 6):
+                uv(1280, 288, j)
+            fin(992, 288, 512)
+            ship(1)
+
+    mine = slice(32 * me, 32 * me + 32)
+    parts = [(lo, hi) for lo, hi in ((0, me), (me + 1, N)) if lo < hi]
+    full = 16 * (2 + len(parts))
+
+    def own(i):
+        a, n = CO[i]
+        dma("g", T.y[mine, a:a + n], T.ON[mine, a:a + n], "gy", full, [reg("ON", a, a + n)], [])
+
+    def slot(r, q):
+        i = [c for c in range(N) if c != r].index(q)
+        return LW * i, LW * i + LW
+    own(0)
+    send("so0", lambda r: T.ly0[me], "ay0", [reg("so0", 0, 4)])
+    arrives("ay0", [reg("ly0", r, r + 1) for r in others], others)
+    own(1)
+    send("so1", lambda r: T.LY[:, slot(r, me)[0]:slot(r, me)[1]], "ay1", [reg("so1", 0, 4)])
+    arrives("ay1", [reg("LY", 0, 3 * LW)], others)
+    a, n = CO[0]
+    for lo, hi in parts:
+        dma("g", T.y[32 * lo:32 * hi, a:a + n], T.ly0[lo:hi], "gy", full, [reg("ly0", lo, hi)], [])
+    copy("v", ("LF", 0, 3 * LW), ("LY", 0, 3 * LW))
+    a, n = CO[1]
+    for i, r in enumerate(others):
+        dma("s" if i == 1 else "y", T.y[32 * r:32 * r + 32, a:a + n], T.LF[:, LW * i:LW * i + LW], "yy", 48,
+            [reg("LF", LW * i, LW * i + LW)], [])
+    for sem in total:
+        if waited.get(sem, 0) < total[sem]:
+            g.wait_ge(T.sem[sem], total[sem])

@@ -2,42 +2,44 @@ from concourse.bass import DstId, RemoteDMATransfer
 from concourse.mybir import AluOpType, ActivationFunctionType
 
 S = 1568
-AC = [(0, 480), (480, 576), (1056, 512)]
-CO = [(0, 992), (992, 576)]
 HALF = 128.500244140625
-LW = CO[1][1] // 4
+PAR = {"A": ((640, None), (608, "pa")), "AO": [(0, 0), (0, 1), (1, 0), (1, 1), (2, 0), (2, 1)], "B": (512, 256), "C": (512, 128), "D": (512, 224), "E": (384, 416), "T": (4, 2), "P": 96, "AL": "pc", "NE": (2, 4)}
+W0 = sum(PAR["E"]) // 4
+BANKS = [(p, a, a + 128) for p in ("pa", "pc", "pd") for a in (0, 512)]
+TURN = [(4 * W0, BANKS[0:PAR["T"][0]]), (S - 128 * PAR["T"][1], BANKS[PAR["T"][0]:sum(PAR["T"])])]
+MID, SLOTS = 12, 25
 
 SCRATCH = {
-    "sx": ("dram", [4, 128, 392], "bfloat16"), "lx": ("dram", [4, 128, 392], "bfloat16"),
-    "se": ("dram", [4, 128, 98], "int32"), "le": ("dram", [4, 128, 98], "int32"),
-    "sl": ("dram", [4, 128, 147], "int32"), "ll": ("dram", [4, 128, 147], "int32"),
-    "E32": ("sbuf", [128, 392], "int32"), "LST": ("sbuf", [128, 392], "uint16"), "CPL": ("sbuf", [128, 588], "uint16"),
-    "IW": ("sbuf", [128, 256], "int32"), "IM": ("sbuf", [128, 16], "int32"), "IB": ("sbuf", [128, 128], "int32"),
-    "JW": ("sbuf", [128, 256], "int32"), "JM": ("sbuf", [128, 16], "int32"), "JB": ("sbuf", [128, 128], "int32"),
-    "W": ("sbuf", [128, 256], "bfloat16"), "NI": ("sbuf", [128, 128], "bfloat16"), "I4": ("sbuf", [128, 128], "bfloat16"),
-    "BO": ("sbuf", [128, 128], "bfloat16"), "MK": ("sbuf", [128, 16], "float32"), "BK": ("sbuf", [128, 2048], "bfloat16"),
-    "RB": ("sbuf", [128, 98], "bfloat16"), "K": ("sbuf", [128, S], "float32"),
-    "N0": ("sbuf", [128, 2048], "bfloat16"), "N1": ("sbuf", [128, 2048], "float32"), "ON": ("sbuf", [128, S], "float16"),
-    "LY": ("sbuf", [128, 3 * LW], "float16"), "LF": ("sbuf", [128, 3 * LW], "float32"),
-    "pa": ("psum", [128, 1024], "float32"), "pb": ("psum", [128, 1024], "float32"), "pk": ("psum", [128, 512], "float32"),
-    "pe0": ("psum", [128, 512], "float32"), "pe1": ("psum", [128, 512], "float32"), "pe2": ("psum", [128, 512], "float32"),
-    "so0": ("dram", [4, 128, CO[0][1] // 4], "float16"), "ly0": ("dram", [4, 128, CO[0][1] // 4], "float16"),
-    "so1": ("dram", [4, 128, LW], "float16"),
+    "zx": ("dram", [SLOTS, 128, 392], "bfloat16"), "ze": ("dram", [SLOTS, 128, 98], "int32"),
+    "zl": ("dram", [SLOTS, 128, 147], "uint16"),
+    "E32": ("sbuf", [128, 354], "int32"), "LST": ("sbuf", [128, 256], "uint16"), "CPL": ("sbuf", [128, 588], "uint16"),
+    "IW": ("sbuf", [128, 128], "int32"), "IB": ("sbuf", [128, 128], "int32"), "JW": ("sbuf", [128, 128], "int32"),
+    "JB": ("sbuf", [128, 128], "bfloat16"),
+    "W": ("sbuf", [128, 256], "bfloat16"), "NI": ("sbuf", [128, 128], "bfloat16"), "WF": ("sbuf", [128, 128], "float32"),
+    "BK": ("sbuf", [128, 2048], "bfloat16"), "RB": ("sbuf", [128, 98], "bfloat16"), "K": ("sbuf", [128, S], "float32"),
+    "N0": ("sbuf", [128, 2048], "bfloat16"), "N1": ("sbuf", [128, 2048], "float32"),
+    "ON0": ("sbuf", [128, 4 * W0], "float16"), "WH": ("sbuf", [128, 128], "float16"),
+    "Z0": ("sbuf", [128, 128 * PAR["T"][0]], "float16"), "Z1": ("sbuf", [128, 128 * PAR["T"][1]], "float16"),
+    "L0": ("sbuf", [128, 128 * PAR["T"][0]], "float16"), "L1": ("sbuf", [128, 128 * PAR["T"][1]], "float16"),
+    "LF": ("sbuf", [128, S], "float32"), "UH": ("sbuf", [128, S], "float16"),
+    "pa": ("psum", [128, 1024], "float32"), "pb": ("psum", [128, 1024], "float32"),
+    "pc": ("psum", [128, 1024], "float32"), "pd": ("psum", [128, 1024], "float32"),
+    "so0": ("dram", [4, 128, W0], "float16"), "ly0": ("dram", [4, 128, W0], "float16"),
 }
 for _s in range(2):
     for _n, _w, _d in (("SE0", 480, "bfloat16"), ("SE1", 480, "bfloat16"), ("SE2", 480, "bfloat16"), ("SE3", 480, "bfloat16"),
-                       ("X1", 480, "bfloat16"), ("X2", 480, "bfloat16"),
-                       ("TA", S, "float32"), ("TP", S, "float32"), ("FA", S, "bfloat16"), ("FB", S, "bfloat16"),
+                       ("X2", S, "bfloat16"),
+                       ("TA", S, "float32"), ("TP", S, "float32"), ("FA", S, "float32"), ("FB", S, "bfloat16"),
                        ("FW", 2064, "bfloat16"), ("UW", 2048, "bfloat16"), ("GW", 2064, "bfloat16"),
-                       ("DG", 3 * S, "bfloat16"), ("DB", S, "float32"), ("VT", S, "bfloat16"), ("VG", 2 * S, "bfloat16"),
+                       ("DG", 3 * S, "bfloat16"), ("DB", S, "float16"), ("VT", S, "bfloat16"), ("VG", 2 * S, "bfloat16"),
                        ("UG", 6 * S, "bfloat16"), ("UA", S, "float32")):
         SCRATCH["%s_%d" % (_n, _s)] = ("sbuf", [128, _w], _d)
 
-SEMAPHORES = (["cv", "cs", "ct", "cg", "rl", "se", "sl", "gx", "gl", "gy", "yy", "EE", "XX", "o0", "o1", "ay0", "ay1"]
-              + ["%s%d" % (a, r) for a in ("ae", "ax", "al") for r in range(4)])
+SEMAPHORES = (["cv", "cs", "ct", "cg", "rl", "se", "sl", "gx", "gy", "ER", "EL", "XA", "XB", "CC", "CP", "o0",
+               "ay0", "az0", "az1", "y0", "y1", "ae", "al"] + ["ax%d" % r for r in range(4)])
 
 
-def masks(src, cores, topo):
+def masks(src, cores, topo, k):
     others = [c for c in cores if c != src]
     eng = dict((c, list(topo.engines(src, c))) for c in others)
     few = min(len(eng[c]) for c in others)
@@ -49,7 +51,17 @@ def masks(src, cores, topo):
         out[c] = eng[c][i * share:(i + 1) * share]
     for c in others:
         if c not in out:
-            out[c] = [e for e in eng[c] if e not in eng[far[0]]][0:4:2]
+            out[c] = [e for e in eng[c] if e not in eng[far[0]]][0:2 * k:2]
+    return out
+
+
+def runs(ranks):
+    out = []
+    for r in sorted(ranks):
+        if out and out[-1][1] == r:
+            out[-1] = (out[-1][0], r + 1)
+        else:
+            out.append((r, r + 1))
     return out
 
 
@@ -65,8 +77,8 @@ def rank_program(g, core, T, topo):
     others = [r for r in range(N) if r != me]
     near = [r for r in others if cores[r] in topo.cores_of(core)]
     order = near + [r for r in others if r not in near]
-    eng = masks(core, cores, topo)
-    inc = dict((r, len(masks(cores[r], cores, topo)[core])) for r in others)
+    engs = [masks(core, cores, topo, k) for k in PAR["NE"]]
+    incs = [dict((r, len(masks(cores[r], cores, topo, k)[core])) for r in others) for k in PAR["NE"]]
 
     queue = {"v": g.vector, "s": g.scalar, "t": g.tensor, "g": g, "y": g.sync}
     total, waited, hist = {}, {}, {}
@@ -123,8 +135,9 @@ def rank_program(g, core, T, topo):
         note(k, rd, wr, (sem, full, dict(know[k]) if full == 16 else {}))
         queue[k].dma_start(out, in_).then_inc(T.sem[sem], 16)
 
-    def send(src, dst, sems, rd):
+    def send(src, dst, sems, rd, wide):
         wait("g", hazards("g", rd, []))
+        eng = engs[wide]
         trs = []
         for r in order:
             rid, pid = topo.addr(cores[r], core)
@@ -132,12 +145,12 @@ def rank_program(g, core, T, topo):
             for e in eng[cores[r]]:
                 m |= 1 << e
             trs.append(RemoteDMATransfer(dst_ids=[DstId(rid=rid, pnc=pid)], dma_engine_mask=m, remote_sem=T.sem[sems],
-                                         src=T[src][r], dst=dst(r)))
+                                         src=src(r), dst=dst(r)))
             total["rl"] = total.get("rl", 0) + len(eng[cores[r]])
         g.remote_dma_fused(trs, local_sem=T.sem["rl"])
 
-    def arrives(sem, regs, srcs):
-        n = sum(inc[r] for r in srcs)
+    def arrives(sem, regs, srcs, wide=0):
+        n = sum(incs[wide][r] for r in srcs)
         total[sem] = total.get(sem, 0) + n
         note("r", [], regs, (sem, n, {}))
 
@@ -147,13 +160,16 @@ def rank_program(g, core, T, topo):
     def ind(win, wn, lst, c0, n):
         return T[win][:, 0:wn].indirect(T[lst][:, c0:c0 + n // 16])
 
-    def pick(k, out, win, wn, lst, c0):
+    def pick(k, out, win, wn, lst, c0, func=None, bias=0.0, scale=1.0):
         n = out[2] - out[1]
         rd = [reg(win, 0, wn), reg(lst, c0, c0 + n // 16)]
         if k == "v":
             op("v", rd, [reg(*out)], lambda: g.vector.tensor_copy(out=ap(out), in_=ind(win, wn, lst, c0, n)))
-        else:
+        elif func is None:
             op("s", rd, [reg(*out)], lambda: g.scalar.activation(out=ap(out), in_=ind(win, wn, lst, c0, n), func=act.Copy))
+        else:
+            op("s", rd, [reg(*out)], lambda: g.scalar.activation(out=ap(out), in_=ind(win, wn, lst, c0, n), func=func,
+                                                                 bias=bias, scale=scale))
 
     def pickop(out, win, wn, lst, c0, other, o):
         n = out[2] - out[1]
@@ -163,19 +179,19 @@ def rank_program(g, core, T, topo):
     def tt(out, a, b, o):
         op("v", [reg(*a), reg(*b)], [reg(*out)], lambda: g.vector.tensor_tensor(out=ap(out), in0=ap(a), in1=ap(b), op=o))
 
-    def ts(out, a, s1, o1, s2=None, o2=None, more=()):
+    def ts(out, a, s1, o1, s2=None, o2=None):
         if o2 is None:
             f = lambda: g.vector.tensor_scalar(out=ap(out), in0=ap(a), scalar1=s1, scalar2=None, op0=o1)
         else:
             f = lambda: g.vector.tensor_scalar(out=ap(out), in0=ap(a), scalar1=s1, scalar2=s2, op0=o1, op1=o2)
-        op("v", [reg(*a)] + list(more), [reg(*out)], f)
+        op("v", [reg(*a)], [reg(*out)], f)
 
-    def actv(out, a, func, bias=0.0, scale=1.0, more=()):
+    def actv(out, a, func, bias=0.0, scale=1.0):
         if func == act.Copy:
             f = lambda: g.scalar.activation(out=ap(out), in_=ap(a), func=func)
         else:
             f = lambda: g.scalar.activation(out=ap(out), in_=ap(a), func=func, bias=bias, scale=scale)
-        op("s", [reg(*a)] + list(more), [reg(*out)], f)
+        op("s", [reg(*a)], [reg(*out)], f)
 
     def copy(k, out, a):
         if k == "v":
@@ -192,200 +208,227 @@ def rank_program(g, core, T, topo):
             m = min(512, n - c)
             mm((pb, p0 + c, p0 + c + m), lhs, (rb, r0 + c, r0 + c + m), start, stop)
 
-    EYE, NEG, I4 = ("W", 0, 128), ("NI", 0, 128), ("I4", 0, 128)
+    EYE, NEG, EYF, EYH = ("W", 0, 128), ("NI", 0, 128), ("WF", 0, 128), ("WH", 0, 128)
 
-    dma("g", T.sx[:], T.x[:], "gx", 16, [], [reg("sx", 0, 4)])
-    for k, j, a, b, t in (("y", 0, 0, 98, T.reac[:, 0:98]), ("s", 3, 0, 30, T.spsend[:]), ("y", 1, 0, 98, T.reac[:, 98:196]),
-                          ("s", 3, 30, 60, T.rxsend[:]), ("y", 2, 0, 98, T.rate[:]),
-                          ("s", 3, 60, 98, T.reac[:, 0:38])):
-        dma(k, T.se[:, j::4, a:b], t, "se", 96, [], [reg("se", 0, 4, 30 * j + a // 30, 30 * j + a // 30 + 1)])
-    for j in range(2):
-        dma("s", T.sl[:, j::4, :], T.cons[:, 147 * j:147 * j + 147], "sl", 64, [], [reg("sl", 0, 4, j, j + 1)])
-        dma("y", T.sl[:, 2 + j::4, :], T.prod[:, 147 * j:147 * j + 147], "sl", 64, [], [reg("sl", 0, 4, 2 + j, 3 + j)])
+    out = slice(MID - me, MID - me + N)
 
-    op("g", [], [reg("IB", 0, 128)], lambda: g.iota(T.IB[:], [[-16, 8], [0, 16]], 128, 1))
-    op("g", [], [reg("IM", 0, 16)], lambda: g.iota(T.IM[:], [[-1, 16]], 128, 1))
-    op("g", [], [reg("IW", 0, 256)], lambda: g.iota(T.IW[:], [[-1, 256]], 256, 1))
-    for a, b, c in (("se", "le", "ae"), ("sx", "lx", "ax"), ("sl", "ll", "al")):
-        send(a, lambda r: T[b][me], "%s%d" % (c, me), [reg(a, 0, 4)])
-        for r in others:
-            arrives("%s%d" % (c, r), [reg(b, r, r + 1)], [r])
+    def inn(lo, hi):
+        return slice(MID + 4 * (lo - me), MID + 4 * (hi - 1 - me) + 1, 4)
+
+    def turn(z, sem, wide=0):
+        send(lambda r: T[z][MID + r - me], lambda r: T[z][MID + 4 * (me - r)], sem, [reg(z, 0, 1)], wide)
+    dma("g", T.zx[out], T.x[:], "gx", 16, [], [reg("zx", 0, 1)])
+    for j, (k, a, b, c, d, t) in enumerate((("y", 96, 128, 0, 30, T.spsend), ("s", 96, 128, 30, 60, T.rxsend),
+                                            ("y", 0, 64, 0, 98, T.reac), ("s", 64, 96, 0, 98, T.rate),
+                                            ("y", 96, 128, 60, 98, T.cons))):
+        dma(k, T.ze[out, a:b, c:d], t[:, 0:38] if c == 60 else t[:], "se", 80, [], [reg("ze", 0, 1, j, j + 1)])
+    turn("ze", "ae")
+    arrives("ae", [reg("ze", 1, 2)], others)
+    turn("zx", "ax%d" % me)
+    for r in others:
+        arrives("ax%d" % r, [reg("zx", 1 + r, 2 + r)], [r])
+
+    op("g", [], [reg("IB", 0, 128)], lambda: g.iota(T.IB[:], [[-16, 8], [0, 16]], 0, 1))
+    op("g", [], [reg("IW", 0, 128)], lambda: g.iota(T.IW[:], [[-1, 128]], 0, 1))
+    for j, t in enumerate((T.cons, T.prod)):
+        dma("g", T.zl[out, 64 * j:64 * j + 64, :], t[:], "sl", 32, [], [reg("zl", 0, 1, j, j + 1)])
+    turn("zl", "al", 1)
+    arrives("al", [reg("zl", 1, 2)], others, 1)
 
     for b in ("FW_0", "GW_0", "FW_1", "GW_1"):
-        op("v", [], [reg(b, 2048, 2064)], lambda: g.vector.memset(T[b][:, 2048:2064], 0.0))
-    ts(("JB", 0, 128), ("IB", 0, 128), 4, AluOpType.arith_shift_right)
-    ts(("JM", 0, 16), ("IM", 0, 16), 15, AluOpType.bitwise_and)
-    ts(("BO", 0, 128), ("JB", 0, 128), 8, eq)
-    ts(("MK", 0, 16), ("JM", 0, 16), 0, eq, 1.0 / 1024, mult)
+        op("v", [], [reg(b, 2048, 2064)], lambda: g.vector.memset(T[b][:, 2048:2064], 129.0 if b[0] == "F" else 0.0))
+    copy("v", ("JB", 0, 128), ("IB", 0, 128))
     for c in range(16):
-        o, m = ("BK", 128 * c, 128 * c + 128), reg("MK", c, c + 1)
-        if c % 2:
-            actv(o, ("BO", 0, 128), act.Identity, 0.0, T.MK[:, c:c + 1], [m])
-        else:
-            ts(o, ("BO", 0, 128), T.MK[:, c:c + 1], mult, None, None, [m])
-    ts(("JW", 0, 256), ("IW", 0, 256), 127, AluOpType.bitwise_and)
-    ts(("W", 0, 256), ("JW", 0, 256), 0, eq)
-    ts(("NI", 0, 128), ("JW", 0, 128), 0, eq, -1, mult)
-    ts(("I4", 0, 128), ("JW", 0, 128), 0, eq, 4, mult)
+        ts(("BK", 128 * c, 128 * c + 128), ("JB", 0, 128), c, eq, 1.0 / 1024, mult)
+    ts(("W", 0, 128), ("IW", 0, 128), 0, eq)
+    ts(("W", 128, 256), ("IW", 0, 128), 0, eq)
+    ts(("NI", 0, 128), ("IW", 0, 128), 0, eq, -1, mult)
+    ts(("WF", 0, 128), ("IW", 0, 128), 0, eq)
+    ts(("WH", 0, 128), ("IW", 0, 128), 0, eq)
 
-    for sem, a, b, buf, n in (("EE", "se", "le", "E32", 392), ("XX", "sx", "lx", "N0", S)):
-        for r in [me] + order:
-            t = a if r == me else b
-            dma("y", T[buf][32 * r:32 * r + 32, 0:n], T[t][r], sem, 64, [reg(t, r, r + 1)], [reg(buf, 0, n, 32 * r, 32 * r + 32)])
-    for r in [me] + order:
-        t = "sl" if r == me else "ll"
-        dma("g", T.CPL[32 * r:32 * r + 32, :], T[t][r], "gl", 64, [reg(t, r, r + 1)], [reg("CPL", 0, 588, 32 * r, 32 * r + 32)])
-    copy("v", ("RB", 0, 98), ("E32", 196, 294))
-    copy("v", ("LST", 0, 354), ("E32", 0, 354))
-
-    def spread(p, p0, c0, c1):
-        for c in range(c0, c1):
-            a = p0 + 98 * (c - c0)
+    RE, SP, RXL = 0, 196, 226
+    every = inn(0, N)
+    dma("y", T.E32[:, 256:354], T.ze[every, 64:96, :], "ER", 16, [reg("ze", 0, 2)], [reg("E32", 256, 354)])
+    for a, b, w, c in ((96, 128, 60, (196, 256)), (0, 64, 98, (0, 196))):
+        dma("s", T.E32[:, c[0]:c[1]], T.ze[every, a:b, 0:w], "EL", 32, [reg("ze", 0, 2)], [reg("E32", c[0], c[1])])
+    for k, sem, rs in (("y", "XA", runs([me] + near)), ("y", "XB", runs([r for r in others if r not in near]))):
+        for lo, hi in rs:
+            dma(k, T.N0[32 * lo:32 * hi, 0:S], T.zx[inn(lo, hi)], sem, 16 * len(rs), [reg("zx", 0, 1), reg("zx", 1 + lo, 1 + hi)],
+                [reg("N0", 0, S, 32 * lo, 32 * hi)])
+    for j, sem in enumerate(("CC", "CP")):
+        dma("y", T.CPL[:, 294 * j:294 * j + 294], T.zl[every, 64 * j:64 * j + 64, :], sem, 16, [reg("zl", 0, 2)],
+            [reg("CPL", 294 * j, 294 * j + 294)])
+    copy("v", ("RB", 0, 98), ("E32", 256, 354))
+    copy("v", ("LST", 0, 256), ("E32", 0, 256))
+    for i, (k, p, p0) in enumerate((("s", "pa", 0), ("v", "pa", 512), ("s", "pb", 0), ("v", "pb", 512))):
+        for c in range(4 * i, 4 * i + 4):
+            a = p0 + 98 * (c % 4)
             mm((p, a, a + 98), ("BK", 128 * c, 128 * c + 128), ("RB", 0, 98), True, True)
-    for k, p, p0, c0, c1 in (("s", "pa", 0, 4, 9), ("v", "pa", 512, 9, 13), ("s", "pb", 0, 13, 16)):
-        spread(p, p0, c0, c1)
-        copy(k, ("K", 98 * c0, 98 * c1), (p, p0, p0 + 98 * (c1 - c0)))
-
-    RE, SP, RXL = 0, 294, 324
+        copy(k, ("K", 392 * i, 392 * i + 392), (p, p0, p0 + 392))
 
     def border(s, e, win, c0):
         se = "SE%d_%d" % (e, s)
-        pick("v", (se, 224, 480), win, S, "LST", c0 + 14)
-        pick("s", (se, 0, 224), win, S, "LST", c0)
-        for m, k in ((2, "s"), (0, "v"), (1, "s")):
-            mm(("pe%d" % m, 0, 160), ("W", 32 * (1 + m), 32 * (1 + m) + 128), (se, 160 * (2 - m), 160 * (3 - m)), True, True)
-            copy(k, (win, S + 160 * m, S + 160 * m + 160), ("pe%d" % m, 0, 160))
+        cut = 320 - PAR["P"]
+        pieces = (("v", 320, 480, "pc", 0), ("s", 0, 160, "pc", 512), ("v", cut, 320, "pd", 0), ("s", 160, cut, "pd", 512))
+        for k, a, b, p, p0 in pieces:
+            m = 2 - a // 160
+            pick(k, (se, a, b), win, S, "LST", c0 + a // 16)
+            mm((p, p0, p0 + b - a), ("W", 32 * (1 + m), 32 * (1 + m) + 128), (se, a, b), True, True)
+        for k, a, b, p, p0 in pieces:
+            m = 2 - a // 160
+            c = S + 160 * m + a % 160
+            copy(k, (win, c, c + b - a), (p, p0, p0 + b - a))
 
     for s in range(2):
         def nm(b):
             return "%s_%d" % (b, s)
         NW, FW, UW, GW = "N%d" % s, nm("FW"), nm("UW"), nm("GW")
+        EN = EYF if s else EYE
         border(s, 0, NW, SP)
-        if s == 0:
-            spread("pk", 0, 0, 5)
+        TA, TP, X2 = nm("TA"), nm("TP"), nm("X2")
+        AC, a = [], 0
+        for n, p in PAR["A"]:
+            AC.append((a, n, p))
+            a += n
+        AC.append((a, S - a, PAR["AL"]))
 
         def kx(i, h):
-            a, n = AC[i]
-            o, x = ((nm("TA"), a, a + n), ("K", a, a + n)) if h == 0 else ((nm("TP"), a, a + n), (nm("TA"), a, a + n))
-            pickop(o, NW, 2048, "LST", RE + 98 * h + a // 16, x, mult)
+            a, n, p = AC[i]
+            if h == 0:
+                pickop((TA, a, a + n), NW, 2048, "LST", RE + a // 16, ("K", a, a + n), mult)
+            elif p:
+                tt((TP, a, a + n), (p, 0, n), (TA, a, a + n), mult)
+            else:
+                pickop((TP, a, a + n), NW, 2048, "LST", RE + 98 + a // 16, (TA, a, a + n), mult)
 
         def whole(i, k):
-            a, n = AC[i]
-            p, fa, fb, f = [(b, a, a + n) for b in (nm("TP"), nm("FA"), nm("FB"), FW)]
+            a, n, p = AC[i]
+            p, fa, f = [(b, a, a + n) for b in (TP, nm("FA"), FW)]
             if k == "s":
-                actv(fa, p, act.Identity, HALF, 1.0)
-                actv(fb, fa, act.Relu, 132.0, -1.0)
-                actv(f, fb, act.Identity, 3.0, -1.0)
+                actv(fa, p, act.Relu, 3.5, -1.0)
+                actv(f, fa, act.Identity, 3.5 + HALF, -1.0)
             else:
-                ts(fa, p, 3.4, amin, HALF, add)
-                ts(f, fa, -129.0, add)
-        n = AC[0][1]
-        pick("s", (nm("X2"), 0, n), NW, 2048, "LST", RE + 98)
-        mm(("pa", 0, n), EYE, (nm("X2"), 0, n), True, True)
-        pick("s", (nm("X1"), 0, n), NW, 2048, "LST", RE)
-        kx(1, 0)
-        kx(1, 1)
-        whole(1, "s")
-        tt((nm("TA"), 0, n), ("pa", 0, n), (nm("X1"), 0, n), mult)
-        tt((nm("TP"), 0, n), ("pk", 0, n), (nm("TA"), 0, n), mult)
-        whole(0, "s")
-        kx(2, 0)
-        kx(2, 1)
-        whole(2, "v")
+                ts(f, p, 3.4, amin, HALF, add)
+        for a, n, p in AC:
+            if p:
+                pick("s", (X2, a, a + n), NW, 2048, "LST", RE + 98 + a // 16)
+                mmw(p, 0, EYE, X2, a, n, True, True)
+        A = sum(PAR["B"])
+        mmw("pb", 0, EN, NW, 0, A, True, False)
+        for i, h in PAR["AO"]:
+            kx(i, h)
+            if h:
+                whole(i, "v" if i == len(AC) - 1 else "s")
         border(s, 1, FW, RXL)
-        DB, DG = nm("DB"), nm("DG")
-        A = 896
-        D = [(0, 608, "pa"), (608, A - 608, "pb")]
-        for a, n, p in D:
-            for c in range(3):
-                pick("s", (DG, S * c + a, S * c + a + n), FW, 2049, "CPL", 98 * c + a // 16)
-                mmw(p, 0, EYE, DG, S * c + a, n, c == 0, c == 2)
+
+        def scalar_part(p, buf, win, wn, lst, c0, signs, a, n0, n1, fin, *fn):
+            for j, sg in enumerate(signs):
+                last = j == len(signs) - 1
+                for b, n in ((0, n0), (n0, n1)) if last else ((0, n0 + n1),):
+                    pick("s", (buf, S * j + a + b, S * j + a + b + n), win, wn, lst, c0 + 98 * j + (a + b) // 16, *fn)
+                    mmw(p, b, sg, buf, S * j + a + b, n, False, last)
+            for b, n in ((0, n0), (n0, n1)):
+                fin(a + b, n, (p, b, b + n))
+        DB = nm("DB")
+        C = S - sum(PAR["C"])
+        mmw("pa", 0, EYE, FW, C, S - C, True, False)
         for c in range(3):
             pickop((DB, A, S), FW, 2049, "CPL", 98 * c + A // 16, (NW if c == 0 else DB, A, S), sub if c == 0 else add)
-        ts((UW, A, S), (DB, A, S), 0.0, le)
-        for a, n, p in D:
-            tt((UW, a, a + n), (p, 0, n), (NW, a, a + n), le)
+            if c == 0:
+                ts((nm("FB"), 0, C), (FW, 0, C), -129.0, add)
+        ts((UW, A, S), (DB, A, S), 3 * 129.0, le, 3.0, mult)
+        scalar_part("pb", nm("DG"), FW, 2049, "CPL", 0, (NEG, NEG, NEG), 0, PAR["B"][0], PAR["B"][1],
+                    lambda a, n, p: actv((UW, a, a + n), p, act.Relu, 3.0 + 9 * 129, 3.0))
         border(s, 2, UW, SP)
-        VT, VG = nm("VT"), nm("VG")
-        A = 960
-        mmw("pb", 0, EYE, FW, A, S - A, True, False)
-        pick("s", (VG, A, S), UW, 2048, "LST", RE + A // 16)
-        mmw("pb", 0, I4, VG, A, S - A, False, False)
-        for a, n in ((A, 512), (A + 512, S - A - 512)):
-            pick("s", (VG, S + a, S + a + n), UW, 2048, "LST", RE + 98 + a // 16)
-            mmw("pb", a - A, I4, VG, S + a, n, False, True)
-        for h in range(2):
-            pickop((VT, 0, A) if h == 0 else (GW, 0, A), UW, 2048, "LST", RE + 98 * h, (FW, 0, A) if h == 0 else (VT, 0, A), mult)
-        for a, n in ((A, 512), (A + 512, S - A - 512)):
-            actv((GW, a, a + n), ("pb", a - A, a - A + n), act.Relu, -8.0, 1.0)
+        VT = nm("VT")
+        e0, e1 = PAR["E"]
+        if s == 0:
+            mmw("pb", 0, EN, NW, 0, sum(PAR["D"]), True, False)
+        else:
+            mm(("pb", 0, e0), EN, (NW, 0, e0), True, False)
+        pickop((VT, 0, C), UW, 2048, "LST", RE, (nm("FB"), 0, C), amin)
+        pickop((GW, 0, C), UW, 2048, "LST", RE + 98, (VT, 0, C), amin)
+        scalar_part("pa", nm("VG"), UW, 2048, "LST", RE, (NEG, NEG), C, PAR["C"][0], PAR["C"][1],
+                    lambda a, n, p: actv((GW, a, a + n), p, act.Relu, -129.0, 1.0), act.Relu, 3.0, -1.0)
         border(s, 3, GW, RXL)
         UA, UG = nm("UA"), nm("UG")
-        out = "N1" if s == 0 else "ON"
+        signs = (NEG, NEG, NEG, EYE, EYE, EYE)
 
-        def uv(a, n, j):
+        def vector_part(a, n, o):
             acc = (UA, a, a + n)
-            pickop((out, a, a + n) if j == 5 else acc, GW, 2049, "CPL", 98 * j + a // 16,
-                   (NW, a, a + n) if j == 0 else acc, sub if j in (0, 3) else add)
-
-        def us(a, n, j, p0):
-            pick("s", (UG, S * j + a, S * j + a + n), GW, 2049, "CPL", 98 * j + a // 16)
-            mmw("pa", p0, NEG if j < 3 else EYE, UG, S * j + a, n, j == 0, j == 5)
-
-        def fin(a, n, p0):
-            tt((out, a, a + n), ("pa", p0, p0 + n), (NW, a, a + n), add)
-
-        def ship(i):
-            a, n = CO[i]
-            dma("y", T["so%d" % i][:], T.ON[:, a:a + n], "o%d" % i, 16, [reg("ON", a, a + n)], [reg("so%d" % i, 0, 4)])
+            for j in range(6):
+                pickop(o if j == 5 else acc, GW, 2049, "CPL", 98 * j + a // 16, (NW, a, a + n) if j == 0 else acc,
+                       sub if j in (0, 3) else add)
         if s == 0:
-            for j in range(5):
-                us(0, 800, j, 0)
-            us(0, 512, 5, 0)
-            us(512, 288, 5, 512)
-            for j in range(6):
-                uv(800, 768, j)
-            fin(0, 512, 0)
-            fin(512, 288, 512)
+            a = sum(PAR["D"])
+            vector_part(a, S - a, ("N1", a, S))
+            scalar_part("pb", UG, GW, 2049, "CPL", 0, signs, 0, PAR["D"][0], PAR["D"][1],
+                        lambda a, n, p: copy("s", ("N1", a, a + n), p))
         else:
+            def us(a, n, j, p0):
+                pick("s", (UG, S * j + a, S * j + a + n), GW, 2049, "CPL", 98 * j + a // 16)
+                mm(("pb", p0, p0 + n), signs[j], (UG, S * j + a, S * j + a + n), False, j == 5)
+
+            def turned(i, k, j):
+                z, banks = TURN[i]
+                n = 128 * len(banks)
+                if k == "s":
+                    o = (UG, S * j + z, S * j + z + n)
+                    pick("s", o, GW, 2049, "CPL", 98 * j + z // 16)
+                else:
+                    o = ("UH" if j == 2 else UA, z, z + n)
+                    pickop(o, GW, 2049, "CPL", 98 * j + z // 16, (UA if j else NW, z, z + n), add if j else sub)
+                for t, p in enumerate(banks if j >= 2 else []):
+                    mm(p, (o[0], o[1] + 128 * t, o[1] + 128 * t + 128), NEG if j > 2 else EYH, j == 3, j == 2)
+
+            def empty(i):
+                nt = len(TURN[i][1])
+                for t, p in enumerate(TURN[i][1]):
+                    o = T["Z%d" % i][:, t::nt]
+                    op("vs"[t % 2], [reg(*p)], [reg("Z%d" % i, 0, 128 * nt, t, t + 1)],
+                       lambda: g.scalar.activation(out=o, in_=ap(p), func=act.Copy) if t % 2 else g.vector.tensor_copy(out=o, in_=ap(p)))
             for j in range(6):
-                us(0, 512, j, 0)
-            for j in range(6):
-                us(992, 288, j, 512)
-            for j in range(6):
-                uv(512, 480, j)
-            uv(1280, 288, 0)
-            fin(0, 512, 0)
-            ship(0)
-            for j in range(1, 6):
-                uv(1280, 288, j)
-            fin(992, 288, 512)
-            ship(1)
+                us(0, e0, j, 0)
+            turned(1, "s", 3)
+            copy("s", ("ON0", 0, e0), ("pb", 0, e0))
+            vector_part(e0, e1, ("ON0", e0, e0 + e1))
+            dma("y", T.so0[:], T.ON0[:], "o0", 16, [reg("ON0", 0, 4 * W0)], [reg("so0", 0, 4)])
+            for i, k, j in ((0, "s", 3), (0, "v", 0), (0, "s", 4), (0, "v", 1), (0, "s", 5), (0, "v", 2), (1, "s", 4), (1, "v", 0), (1, "v", 1)):
+                turned(i, k, j)
+            empty(0)
+            for k, j in (("s", 5), ("v", 2)):
+                turned(1, k, j)
+            empty(1)
 
     mine = slice(32 * me, 32 * me + 32)
-    parts = [(lo, hi) for lo, hi in ((0, me), (me + 1, N)) if lo < hi]
-    full = 16 * (2 + len(parts))
-
-    def own(i):
-        a, n = CO[i]
-        dma("g", T.y[mine, a:a + n], T.ON[mine, a:a + n], "gy", full, [reg("ON", a, a + n)], [])
-
-    def slot(r, q):
-        i = [c for c in range(N) if c != r].index(q)
-        return LW * i, LW * i + LW
-    own(0)
-    send("so0", lambda r: T.ly0[me], "ay0", [reg("so0", 0, 4)])
-    arrives("ay0", [reg("ly0", r, r + 1) for r in others], others)
-    own(1)
-    send("so1", lambda r: T.LY[:, slot(r, me)[0]:slot(r, me)[1]], "ay1", [reg("so1", 0, 4)])
-    arrives("ay1", [reg("LY", 0, 3 * LW)], others)
-    a, n = CO[0]
+    parts = runs(others)
+    a = 4 * W0
+    full = 16 * (1 + len(parts))
+    dma("g", T.y[mine, 0:a], T.ON0[mine, :], "gy", full, [reg("ON0", 0, a)], [])
+    send(lambda r: T.so0[r], lambda r: T.ly0[me], "ay0", [reg("so0", 0, 4)], 1)
+    arrives("ay0", [reg("ly0", 0, N)], others, 1)
+    for i in range(2):
+        z, l, w = "Z%d" % i, "L%d" % i, 32 * len(TURN[i][1])
+        send(lambda r: T[z][:, w * r:w * r + w], lambda r: T[l][:, w * me:w * me + w], "az%d" % i, [reg(z, 0, 4 * w)], 1)
+        arrives("az%d" % i, [reg(l, w * r, w * r + w) for r in others], others, 1)
+        copy("v", (l, w * me, w * me + w), (z, w * me, w * me + w))
     for lo, hi in parts:
-        dma("g", T.y[32 * lo:32 * hi, a:a + n], T.ly0[lo:hi], "gy", full, [reg("ly0", lo, hi)], [])
-    copy("v", ("LF", 0, 3 * LW), ("LY", 0, 3 * LW))
-    a, n = CO[1]
-    for i, r in enumerate(others):
-        dma("s" if i == 1 else "y", T.y[32 * r:32 * r + 32, a:a + n], T.LF[:, LW * i:LW * i + LW], "yy", 48,
-            [reg("LF", LW * i, LW * i + LW)], [])
+        dma("g", T.y[32 * lo:32 * hi, 0:a], T.ly0[lo:hi], "gy", full, [reg("ly0", lo, hi)], [])
+    for i, p in enumerate(("pb", "pa")):
+        z, nt = TURN[i][0], len(TURN[i][1])
+        half = [(0, (nt + 1) // 2), ((nt + 1) // 2, nt)]
+        for h, (lo, hi) in enumerate(half):
+            for t in range(lo, hi):
+                o = (p, 512 * h + 128 * (t - lo), 512 * h + 128 * (t - lo) + 128)
+                op("t", [reg("L%d" % i, 0, 128 * nt), reg(*EYH)], [reg(*o)],
+                   lambda: g.tensor.matmul(out=ap(o), lhsT=T["L%d" % i][:, t::nt], rhs=ap(EYH), start=True, stop=True))
+        for h, (lo, hi) in enumerate(half):
+            o, q = ("LF", z + 128 * lo, z + 128 * hi), (p, 512 * h, 512 * h + 128 * (hi - lo))
+            if h:
+                actv(o, q, act.Identity, 0.0, -1.0)
+            else:
+                ts(o, q, -1.0, mult)
+        dma("y", T.y[:, z:z + 128 * nt], T.LF[:, z:z + 128 * nt], "y%d" % i, 16, [reg("LF", z, z + 128 * nt)], [])
     for sem in total:
         if waited.get(sem, 0) < total[sem]:
             g.wait_ge(T.sem[sem], total[sem])

@@ -3,20 +3,22 @@ from concourse.mybir import AluOpType, ActivationFunctionType
 
 S = 1568
 HALF = 128.500244140625
-PAR = {"A": ((640, None), (608, "pa")), "AO": [(0, 0), (0, 1), (1, 0), (1, 1), (2, 0), (2, 1)], "B": (512, 256), "C": (512, 128), "D": (512, 224), "E": (384, 416), "T": (4, 2), "P": 96, "AL": "pc", "NE": (2, 4)}
+PAR = {"A": ((512, None), (640, "pa")), "AO": [(0, 0), (0, 1), (1, 0), (1, 1), (2, 0), (2, 1)], "B": (512, 256), "C": (512, 224), "D": (512, 224), "E": (384, 416), "T": (4, 2), "G": 1, "P": ((("v", 320, 480), 320, 480), (("s", 0, 224), 0, 160), (("v", 224, 320), 160, 320)), "BC": ((0, "v"), (1, "s"), (2, "v")), "M": {2: "sv", 3: "ss", 6: "ss"}, "FZ": 256, "AC": 416, "IL": 2, "AL": "pc", "NE": (1, 4)}
 W0 = sum(PAR["E"]) // 4
-BANKS = [(p, a, a + 128) for p in ("pa", "pc", "pd") for a in (0, 512)]
+BANKS = [(p, a, a + 128) for p in ("pa", "pc", "pd", "pb") for a in (512, 0)]
 TURN = [(4 * W0, BANKS[0:PAR["T"][0]]), (S - 128 * PAR["T"][1], BANKS[PAR["T"][0]:sum(PAR["T"])])]
 MID, SLOTS = 12, 25
 
 SCRATCH = {
-    "zx": ("dram", [SLOTS, 128, 392], "bfloat16"), "ze": ("dram", [SLOTS, 128, 98], "int32"),
+    "ze": ("dram", [SLOTS, 128, 64], "int32"), "zr": ("dram", [SLOTS, 128, 32], "int32"),
     "zl": ("dram", [SLOTS, 128, 147], "uint16"),
+    "X32": ("sbuf", [128, S], "int32"), "XO": ("sbuf", [128, S], "int32"), "X16": ("sbuf", [128, S], "bfloat16"),
+    "XL": ("sbuf", [128, S], "bfloat16"),
     "E32": ("sbuf", [128, 354], "int32"), "LST": ("sbuf", [128, 256], "uint16"), "CPL": ("sbuf", [128, 588], "uint16"),
     "IW": ("sbuf", [128, 128], "int32"), "IB": ("sbuf", [128, 128], "int32"), "JW": ("sbuf", [128, 128], "int32"),
     "JB": ("sbuf", [128, 128], "bfloat16"),
     "W": ("sbuf", [128, 256], "bfloat16"), "NI": ("sbuf", [128, 128], "bfloat16"), "WF": ("sbuf", [128, 128], "float32"),
-    "BK": ("sbuf", [128, 2048], "bfloat16"), "RB": ("sbuf", [128, 98], "bfloat16"), "K": ("sbuf", [128, S], "float32"),
+    "BK": ("sbuf", [128, 2048], "bfloat16"), "RB": ("sbuf", [128, 98], "bfloat16"), "K": ("sbuf", [128, 512], "float32"),
     "N0": ("sbuf", [128, 2048], "bfloat16"), "N1": ("sbuf", [128, 2048], "float32"),
     "ON0": ("sbuf", [128, 4 * W0], "float16"), "WH": ("sbuf", [128, 128], "float16"),
     "Z0": ("sbuf", [128, 128 * PAR["T"][0]], "float16"), "Z1": ("sbuf", [128, 128 * PAR["T"][1]], "float16"),
@@ -24,7 +26,7 @@ SCRATCH = {
     "LF": ("sbuf", [128, S], "float32"), "UH": ("sbuf", [128, S], "float16"),
     "pa": ("psum", [128, 1024], "float32"), "pb": ("psum", [128, 1024], "float32"),
     "pc": ("psum", [128, 1024], "float32"), "pd": ("psum", [128, 1024], "float32"),
-    "so0": ("dram", [4, 128, W0], "float16"), "ly0": ("dram", [4, 128, W0], "float16"),
+    "zo": ("dram", [SLOTS, 128, W0], "float16"),
 }
 for _s in range(2):
     for _n, _w, _d in (("SE0", 480, "bfloat16"), ("SE1", 480, "bfloat16"), ("SE2", 480, "bfloat16"), ("SE3", 480, "bfloat16"),
@@ -35,8 +37,8 @@ for _s in range(2):
                        ("UG", 6 * S, "bfloat16"), ("UA", S, "float32")):
         SCRATCH["%s_%d" % (_n, _s)] = ("sbuf", [128, _w], _d)
 
-SEMAPHORES = (["cv", "cs", "ct", "cg", "rl", "se", "sl", "gx", "gy", "ER", "EL", "XA", "XB", "CC", "CP", "o0",
-               "ay0", "az0", "az1", "y0", "y1", "ae", "al"] + ["ax%d" % r for r in range(4)])
+SEMAPHORES = (["cv", "cs", "ct", "cg", "rl", "se", "sl", "gy", "ER", "EL", "EX", "CC", "CP", "o0",
+               "ay0", "az0", "az1", "y0", "y1", "ae", "al", "ar", "sr", "ES"] + ["%s%d" % (a, r) for a in ("ax", "gx") for r in range(4)])
 
 
 def masks(src, cores, topo, k):
@@ -48,7 +50,7 @@ def masks(src, cores, topo, k):
     share = 1 << (share.bit_length() - 1)
     out = {}
     for i, c in enumerate(far):
-        out[c] = eng[c][i * share:(i + 1) * share]
+        out[c] = eng[c][i * share:(i + 1) * share][0:k]
     for c in others:
         if c not in out:
             out[c] = [e for e in eng[c] if e not in eng[far[0]]][0:2 * k:2]
@@ -135,18 +137,17 @@ def rank_program(g, core, T, topo):
         note(k, rd, wr, (sem, full, dict(know[k]) if full == 16 else {}))
         queue[k].dma_start(out, in_).then_inc(T.sem[sem], 16)
 
-    def send(src, dst, sems, rd, wide):
+    def send(src, dst, sems, rd, wide, to=order):
         wait("g", hazards("g", rd, []))
         eng = engs[wide]
         trs = []
-        for r in order:
+        for r in to:
             rid, pid = topo.addr(cores[r], core)
-            m = 0
-            for e in eng[cores[r]]:
-                m |= 1 << e
-            trs.append(RemoteDMATransfer(dst_ids=[DstId(rid=rid, pnc=pid)], dma_engine_mask=m, remote_sem=T.sem[sems],
-                                         src=src(r), dst=dst(r)))
-            total["rl"] = total.get("rl", 0) + len(eng[cores[r]])
+            bits = [1 << e for e in eng[cores[r]]]
+            for m, a, b in zip(bits, src, dst) if isinstance(src, list) else ((sum(bits), src, dst),):
+                trs.append(RemoteDMATransfer(dst_ids=[DstId(rid=rid, pnc=pid)], dma_engine_mask=m, remote_sem=T.sem[sems],
+                                             src=a(r), dst=b(r)))
+            total["rl"] = total.get("rl", 0) + len(bits)
         g.remote_dma_fused(trs, local_sem=T.sem["rl"])
 
     def arrives(sem, regs, srcs, wide=0):
@@ -217,64 +218,121 @@ def rank_program(g, core, T, topo):
 
     def turn(z, sem, wide=0):
         send(lambda r: T[z][MID + r - me], lambda r: T[z][MID + 4 * (me - r)], sem, [reg(z, 0, 1)], wide)
-    dma("g", T.zx[out], T.x[:], "gx", 16, [], [reg("zx", 0, 1)])
-    for j, (k, a, b, c, d, t) in enumerate((("y", 96, 128, 0, 30, T.spsend), ("s", 96, 128, 30, 60, T.rxsend),
-                                            ("y", 0, 64, 0, 98, T.reac), ("s", 64, 96, 0, 98, T.rate),
-                                            ("y", 96, 128, 60, 98, T.cons))):
-        dma(k, T.ze[out, a:b, c:d], t[:, 0:38] if c == 60 else t[:], "se", 80, [], [reg("ze", 0, 1, j, j + 1)])
-    turn("ze", "ae")
-    arrives("ae", [reg("ze", 1, 2)], others)
-    turn("zx", "ax%d" % me)
-    for r in others:
-        arrives("ax%d" % r, [reg("zx", 1 + r, 2 + r)], [r])
-
     op("g", [], [reg("IB", 0, 128)], lambda: g.iota(T.IB[:], [[-16, 8], [0, 16]], 0, 1))
     op("g", [], [reg("IW", 0, 128)], lambda: g.iota(T.IW[:], [[-1, 128]], 0, 1))
-    for j, t in enumerate((T.cons, T.prod)):
-        dma("g", T.zl[out, 64 * j:64 * j + 64, :], t[:], "sl", 32, [], [reg("zl", 0, 1, j, j + 1)])
-    turn("zl", "al", 1)
-    arrives("al", [reg("zl", 1, 2)], others, 1)
-
     for b in ("FW_0", "GW_0", "FW_1", "GW_1"):
         op("v", [], [reg(b, 2048, 2064)], lambda: g.vector.memset(T[b][:, 2048:2064], 129.0 if b[0] == "F" else 0.0))
     copy("v", ("JB", 0, 128), ("IB", 0, 128))
     for c in range(16):
         ts(("BK", 128 * c, 128 * c + 128), ("JB", 0, 128), c, eq, 1.0 / 1024, mult)
+    for k, a, b, t in (("y", 0, 98, T.rate), ("s", 98, 128, T.spsend)):
+        dma(k, T.zr[out, a:b, :], t[:], "sr", 32, [], [reg("zr", 0, 1, a, b)])
+    far = [r for r in others if r not in near]
+    for r in far + near:
+        a, b = 392 * r, 392 * r + 392
+        for j in range(4):
+            dma("ys"[j % 2], T.X32[32 * j:32 * j + 32, a:b], T.x[32 * r:32 * r + 32, 392 * j:392 * j + 392], "gx%d" % r, 64, [],
+                [reg("X32", a, b, 32 * j, 32 * j + 32)])
+        copy("v", ("X16", a, b), ("X32", a, b))
+    mine = slice(32 * me, 32 * me + 32)
+    dma("y", T.XO[mine, :], T.x[mine, :], "gx%d" % me, 16, [], [reg("XO", 0, S)])
+    op("v", [reg("XO", 0, S)], [reg("N0", 0, S, 32 * me, 32 * me + 32)],
+       lambda: g.vector.tensor_copy(out=T.N0[mine, 0:S], in_=T.XO[mine, :]))
+    for k, a, b, t in (("y", 0, 98, T.reac), ("s", 98, 113, T.rxsend), ("s", 113, 128, T.rxsend)):
+        dma(k, T.ze[out, a:b, :], t[:], "se", 48, [], [reg("ze", 0, 1, a, b)])
+    turn("zr", "ar")
+    arrives("ar", [reg("zr", 1, 2)], others)
+
+    def spread(p, p0, a, b, rb="RB"):
+        while a < b:
+            c = a // 98
+            n = min(b - a, 98 * (c + 1) - a, 512 - p0 % 512)
+            mm((p, p0, p0 + n), ("BK", 128 * c, 128 * c + 128), (rb, a - 98 * c, a - 98 * c + n), True, True)
+            a, p0 = a + n, p0 + n
+    for to in (far, near):
+        send(lambda r: T.X16[:, 392 * r:392 * r + 392], lambda r: T.XL[:, 392 * me:392 * me + 392], "ax%d" % me,
+             [reg("X16", 392 * r, 392 * r + 392) for r in to], 1, to)
+    for r in others:
+        arrives("ax%d" % r, [reg("XL", 392 * r, 392 * r + 392)], [r], 1)
+    turn("ze", "ae", 1)
+    arrives("ae", [reg("ze", 1, 2)], others, 1)
+    for j, t in enumerate((T.cons, T.prod)):
+        dma("g", T.zl[out, 64 * j:64 * j + 64, :], t[:], "sl", 32, [], [reg("zl", 0, 1, j, j + 1)])
+    turn("zl", "al", 1)
+    arrives("al", [reg("zl", 1, 2)], others, 1)
     ts(("W", 0, 128), ("IW", 0, 128), 0, eq)
     ts(("W", 128, 256), ("IW", 0, 128), 0, eq)
     ts(("NI", 0, 128), ("IW", 0, 128), 0, eq, -1, mult)
     ts(("WF", 0, 128), ("IW", 0, 128), 0, eq)
     ts(("WH", 0, 128), ("IW", 0, 128), 0, eq)
 
-    RE, SP, RXL = 0, 196, 226
+    RE, SP, RXL = 0, 226, 196
     every = inn(0, N)
-    dma("y", T.E32[:, 256:354], T.ze[every, 64:96, :], "ER", 16, [reg("ze", 0, 2)], [reg("E32", 256, 354)])
-    for a, b, w, c in ((96, 128, 60, (196, 256)), (0, 64, 98, (0, 196))):
-        dma("s", T.E32[:, c[0]:c[1]], T.ze[every, a:b, 0:w], "EL", 32, [reg("ze", 0, 2)], [reg("E32", c[0], c[1])])
-    for k, sem, rs in (("y", "XA", runs([me] + near)), ("y", "XB", runs([r for r in others if r not in near]))):
-        for lo, hi in rs:
-            dma(k, T.N0[32 * lo:32 * hi, 0:S], T.zx[inn(lo, hi)], sem, 16 * len(rs), [reg("zx", 0, 1), reg("zx", 1 + lo, 1 + hi)],
-                [reg("N0", 0, S, 32 * lo, 32 * hi)])
+    dma("y", T.E32[:, 256:354], T.zr[every, 0:98, :], "ER", 16, [reg("zr", 0, 2)], [reg("E32", 256, 354)])
+    dma("s", T.E32[:, 226:256], T.zr[every, 98:128, :], "ES", 16, [reg("zr", 0, 2)], [reg("E32", 226, 256)])
+    for sem, a, b, c, d in (("EL", 0, 98, 0, 196), ("EX", 98, 113, 196, 226)):
+        dma("y", T.E32[:, c:d], T.ze[every, a:b, :], sem, 16, [reg("ze", 0, 2)], [reg("E32", c, d)])
     for j, sem in enumerate(("CC", "CP")):
         dma("y", T.CPL[:, 294 * j:294 * j + 294], T.zl[every, 64 * j:64 * j + 64, :], sem, 16, [reg("zl", 0, 2)],
             [reg("CPL", 294 * j, 294 * j + 294)])
+
+    def wanted(s, win, lst, chunks, fw, between=None):
+        for a, n, k in chunks:
+            if k[0] != "K":
+                pick("s", ("X2_%d" % s, a, a + n), win, 2048, lst, 98 + a // 16)
+        both = S - PAR["AC"]
+        if both < S:
+            pick("s", ("VT_%d" % s, both, S), win, 2048, lst, both // 16)
+            mm(("pd", 0, S - both), EYE, ("VT_%d" % s, both, S), True, True)
+        between()
+        for i, (a, n, k) in enumerate(chunks):
+            ta, tp, fa, x2 = [("%s_%d" % (b, s), a, a + n) for b in ("TA", "TP", "FA", "X2")]
+            k, f = (k[0], k[1], k[1] + n), (fw, a, a + n)
+            if k[0] == "K":
+                pickop(ta, win, 2048, lst, a // 16, k, mult)
+                pickop(tp, win, 2048, lst, 98 + a // 16, ta, mult)
+            else:
+                b = min(a + n, max(a, both))
+                if a < b:
+                    pickop((ta[0], a, b), win, 2048, lst, a // 16, (x2[0], a, b), mult)
+                if b < a + n:
+                    tt((ta[0], b, a + n), ("pd", b - both, a + n - both), (x2[0], b, a + n), mult)
+                tt(tp, k, ta, mult)
+            if s + i == 0:
+                copy("v", ("LST", 196, 226), ("E32", 196, 226))
+            if i < len(chunks) - 1:
+                actv(fa, tp, act.Relu, 3.5, -1.0)
+                actv(f, fa, act.Identity, 3.5 + HALF, -1.0)
+            else:
+                ts(f, tp, 3.4, amin, HALF, add)
+
+    def place(r, ks):
+        for j, k in enumerate(ks):
+            o, i = T.N0[32 * r:32 * r + 32, 392 * j:392 * j + 392], T.XL[32 * j:32 * j + 32, 392 * r:392 * r + 392]
+            op(k, [reg("XL", 392 * r, 392 * r + 392)], [reg("N0", 392 * j, 392 * j + 392, 32 * r, 32 * r + 32)],
+               lambda: g.vector.tensor_copy(out=o, in_=i) if k == "v" else g.scalar.activation(out=o, in_=i, func=act.Copy))
+    for r, ks in zip(near + far, ("vvvs", "vvss")):
+        place(r, ks)
     copy("v", ("RB", 0, 98), ("E32", 256, 354))
-    copy("v", ("LST", 0, 256), ("E32", 0, 256))
-    for i, (k, p, p0) in enumerate((("s", "pa", 0), ("v", "pa", 512), ("s", "pb", 0), ("v", "pb", 512))):
-        for c in range(4 * i, 4 * i + 4):
-            a = p0 + 98 * (c % 4)
-            mm((p, a, a + 98), ("BK", 128 * c, 128 * c + 128), ("RB", 0, 98), True, True)
-        copy(k, ("K", 392 * i, 392 * i + 392), (p, p0, p0 + 392))
+    KA, KL = PAR["A"][0][0], sum(n for n, p in PAR["A"])
+    spread("pb", 0, 0, KA)
+    place(far[-1], "vvvs")
+    copy("v", ("LST", 226, 256), ("E32", 226, 256))
 
     def border(s, e, win, c0):
         se = "SE%d_%d" % (e, s)
-        cut = 320 - PAR["P"]
-        pieces = (("v", 320, 480, "pc", 0), ("s", 0, 160, "pc", 512), ("v", cut, 320, "pd", 0), ("s", 160, cut, "pd", 512))
+        pieces = [x + y for x, y in zip(PAR["P"], (("pc", 0), ("pc", 512), ("pd", 0), ("pd", 512)))]
         for k, a, b, p, p0 in pieces:
             m = 2 - a // 160
-            pick(k, (se, a, b), win, S, "LST", c0 + a // 16)
+            if k:
+                pick(k[0], (se, k[1], k[2]), win, S, "LST", c0 + k[1] // 16)
             mm((p, p0, p0 + b - a), ("W", 32 * (1 + m), 32 * (1 + m) + 128), (se, a, b), True, True)
-        for k, a, b, p, p0 in pieces:
+        if s + e == 0:
+            copy("s", ("K", 0, KA), ("pb", 0, KA))
+        if e == 1 and PAR["FZ"]:
+            actv(("FB_%d" % s, 0, PAR["FZ"]), (win, 0, PAR["FZ"]), act.Identity, -129.0, 1.0)
+        for i, k in PAR["BC"]:
+            a, b, p, p0 = pieces[i][1:]
             m = 2 - a // 160
             c = S + 160 * m + a % 160
             copy(k, (win, c, c + b - a), (p, p0, p0 + b - a))
@@ -285,40 +343,13 @@ def rank_program(g, core, T, topo):
         NW, FW, UW, GW = "N%d" % s, nm("FW"), nm("UW"), nm("GW")
         EN = EYF if s else EYE
         border(s, 0, NW, SP)
-        TA, TP, X2 = nm("TA"), nm("TP"), nm("X2")
-        AC, a = [], 0
-        for n, p in PAR["A"]:
-            AC.append((a, n, p))
-            a += n
-        AC.append((a, S - a, PAR["AL"]))
-
-        def kx(i, h):
-            a, n, p = AC[i]
-            if h == 0:
-                pickop((TA, a, a + n), NW, 2048, "LST", RE + a // 16, ("K", a, a + n), mult)
-            elif p:
-                tt((TP, a, a + n), (p, 0, n), (TA, a, a + n), mult)
-            else:
-                pickop((TP, a, a + n), NW, 2048, "LST", RE + 98 + a // 16, (TA, a, a + n), mult)
-
-        def whole(i, k):
-            a, n, p = AC[i]
-            p, fa, f = [(b, a, a + n) for b in (TP, nm("FA"), FW)]
-            if k == "s":
-                actv(fa, p, act.Relu, 3.5, -1.0)
-                actv(f, fa, act.Identity, 3.5 + HALF, -1.0)
-            else:
-                ts(f, p, 3.4, amin, HALF, add)
-        for a, n, p in AC:
-            if p:
-                pick("s", (X2, a, a + n), NW, 2048, "LST", RE + 98 + a // 16)
-                mmw(p, 0, EYE, X2, a, n, True, True)
         A = sum(PAR["B"])
-        mmw("pb", 0, EN, NW, 0, A, True, False)
-        for i, h in PAR["AO"]:
-            kx(i, h)
-            if h:
-                whole(i, "v" if i == len(AC) - 1 else "s")
+        if s == 0:
+            copy("v", ("LST", 0, 196), ("E32", 0, 196))
+            spread("pa", 0, KA, KL)
+        spread("pc", 0, KL, S)
+        wanted(s, NW, "LST", [(0, KA, ("K", 0)), (KA, KL - KA, ("pa", 0)), (KL, S - KL, ("pc", 0))], FW,
+               lambda: mmw("pb", 0, EN, NW, 0, A, True, False))
         border(s, 1, FW, RXL)
 
         def scalar_part(p, buf, win, wn, lst, c0, signs, a, n0, n1, fin, *fn):
@@ -327,43 +358,47 @@ def rank_program(g, core, T, topo):
                 for b, n in ((0, n0), (n0, n1)) if last else ((0, n0 + n1),):
                     pick("s", (buf, S * j + a + b, S * j + a + b + n), win, wn, lst, c0 + 98 * j + (a + b) // 16, *fn)
                     mmw(p, b, sg, buf, S * j + a + b, n, False, last)
-            for b, n in ((0, n0), (n0, n1)):
-                fin(a + b, n, (p, b, b + n))
+            m = PAR["M"][len(signs)]
+            fin(m[0], a, n0, (p, 0, n0))
+            fin(m[1], a + n0, n1, (p, n0, n0 + n1))
         DB = nm("DB")
         C = S - sum(PAR["C"])
         mmw("pa", 0, EYE, FW, C, S - C, True, False)
         for c in range(3):
             pickop((DB, A, S), FW, 2049, "CPL", 98 * c + A // 16, (NW if c == 0 else DB, A, S), sub if c == 0 else add)
             if c == 0:
-                ts((nm("FB"), 0, C), (FW, 0, C), -129.0, add)
+                ts((nm("FB"), PAR["FZ"], C), (FW, PAR["FZ"], C), -129.0, add)
         ts((UW, A, S), (DB, A, S), 3 * 129.0, le, 3.0, mult)
         scalar_part("pb", nm("DG"), FW, 2049, "CPL", 0, (NEG, NEG, NEG), 0, PAR["B"][0], PAR["B"][1],
-                    lambda a, n, p: actv((UW, a, a + n), p, act.Relu, 3.0 + 9 * 129, 3.0))
+                    lambda k, a, n, p: actv((UW, a, a + n), p, act.Relu, 3.0 + 9 * 129, 3.0) if k == "s" else
+                    ts((UW, a, a + n), p, -3 * 129.0, AluOpType.is_ge, 3.0, mult))
         border(s, 2, UW, SP)
         VT = nm("VT")
         e0, e1 = PAR["E"]
         if s == 0:
             mmw("pb", 0, EN, NW, 0, sum(PAR["D"]), True, False)
-        else:
-            mm(("pb", 0, e0), EN, (NW, 0, e0), True, False)
         pickop((VT, 0, C), UW, 2048, "LST", RE, (nm("FB"), 0, C), amin)
         pickop((GW, 0, C), UW, 2048, "LST", RE + 98, (VT, 0, C), amin)
         scalar_part("pa", nm("VG"), UW, 2048, "LST", RE, (NEG, NEG), C, PAR["C"][0], PAR["C"][1],
-                    lambda a, n, p: actv((GW, a, a + n), p, act.Relu, -129.0, 1.0), act.Relu, 3.0, -1.0)
+                    lambda k, a, n, p: actv((GW, a, a + n), p, act.Relu, -129.0, 1.0) if k == "s" else
+                    ts((GW, a, a + n), p, -129.0, add, 0.0, AluOpType.max), act.Relu, 3.0, -1.0)
         border(s, 3, GW, RXL)
         UA, UG = nm("UA"), nm("UG")
         signs = (NEG, NEG, NEG, EYE, EYE, EYE)
 
         def vector_part(a, n, o):
-            acc = (UA, a, a + n)
+            h = n // 64 * 32 if PAR["IL"] > s else n
             for j in range(6):
-                pickop(o if j == 5 else acc, GW, 2049, "CPL", 98 * j + a // 16, (NW, a, a + n) if j == 0 else acc,
-                       sub if j in (0, 3) else add)
+                for b, c in ((0, h), (h, n)) if h < n else ((0, n),):
+                    acc = (UA, a + b, a + c)
+                    pickop((o[0], o[1] + b, o[1] + c) if j == 5 else acc, GW, 2049, "CPL", 98 * j + (a + b) // 16,
+                           (NW, a + b, a + c) if j == 0 else acc, sub if j in (0, 3) else add)
         if s == 0:
+            spread("pa", 0, KA, KL)
             a = sum(PAR["D"])
             vector_part(a, S - a, ("N1", a, S))
             scalar_part("pb", UG, GW, 2049, "CPL", 0, signs, 0, PAR["D"][0], PAR["D"][1],
-                        lambda a, n, p: copy("s", ("N1", a, a + n), p))
+                        lambda k, a, n, p: copy(k, ("N1", a, a + n), p))
         else:
             def us(a, n, j, p0):
                 pick("s", (UG, S * j + a, S * j + a + n), GW, 2049, "CPL", 98 * j + a // 16)
@@ -378,8 +413,10 @@ def rank_program(g, core, T, topo):
                 else:
                     o = ("UH" if j == 2 else UA, z, z + n)
                     pickop(o, GW, 2049, "CPL", 98 * j + z // 16, (UA if j else NW, z, z + n), add if j else sub)
+                if (i, j) == (1, 3):
+                    copy("s", ("ON0", 0, e0), ("pb", 0, e0))
                 for t, p in enumerate(banks if j >= 2 else []):
-                    mm(p, (o[0], o[1] + 128 * t, o[1] + 128 * t + 128), NEG if j > 2 else EYH, j == 3, j == 2)
+                    mm(p, (o[0], o[1] + 128 * t, o[1] + 128 * t + 128), NEG if j > 2 else EYH, j == 3, j == 5)
 
             def empty(i):
                 nt = len(TURN[i][1])
@@ -387,34 +424,28 @@ def rank_program(g, core, T, topo):
                     o = T["Z%d" % i][:, t::nt]
                     op("vs"[t % 2], [reg(*p)], [reg("Z%d" % i, 0, 128 * nt, t, t + 1)],
                        lambda: g.scalar.activation(out=o, in_=ap(p), func=act.Copy) if t % 2 else g.vector.tensor_copy(out=o, in_=ap(p)))
+            mm(("pb", 0, e0), EN, (NW, 0, e0), True, False)
             for j in range(6):
                 us(0, e0, j, 0)
             turned(1, "s", 3)
-            copy("s", ("ON0", 0, e0), ("pb", 0, e0))
             vector_part(e0, e1, ("ON0", e0, e0 + e1))
-            dma("y", T.so0[:], T.ON0[:], "o0", 16, [reg("ON0", 0, 4 * W0)], [reg("so0", 0, 4)])
-            for i, k, j in ((0, "s", 3), (0, "v", 0), (0, "s", 4), (0, "v", 1), (0, "s", 5), (0, "v", 2), (1, "s", 4), (1, "v", 0), (1, "v", 1)):
+            dma("y", T.zo[out], T.ON0[:], "o0", 16, [reg("ON0", 0, 4 * W0)], [reg("zo", 0, 1)])
+            for i, k, j in ((0, "s", 3), (0, "v", 0), (0, "s", 4), (0, "v", 1), (0, "v", 2), (0, "s", 5), (1, "s", 4), (1, "v", 0), (1, "v", 1)):
                 turned(i, k, j)
             empty(0)
-            for k, j in (("s", 5), ("v", 2)):
+            for k, j in (("v", 2), ("s", 5)):
                 turned(1, k, j)
             empty(1)
 
-    mine = slice(32 * me, 32 * me + 32)
-    parts = runs(others)
-    a = 4 * W0
-    full = 16 * (1 + len(parts))
-    dma("g", T.y[mine, 0:a], T.ON0[mine, :], "gy", full, [reg("ON0", 0, a)], [])
-    send(lambda r: T.so0[r], lambda r: T.ly0[me], "ay0", [reg("so0", 0, 4)], 1)
-    arrives("ay0", [reg("ly0", 0, N)], others, 1)
+    turn("zo", "ay0", 1)
+    arrives("ay0", [reg("zo", 1, 2)], others, 1)
     for i in range(2):
         z, l, w = "Z%d" % i, "L%d" % i, 32 * len(TURN[i][1])
         send(lambda r: T[z][:, w * r:w * r + w], lambda r: T[l][:, w * me:w * me + w], "az%d" % i, [reg(z, 0, 4 * w)], 1)
         arrives("az%d" % i, [reg(l, w * r, w * r + w) for r in others], others, 1)
         copy("v", (l, w * me, w * me + w), (z, w * me, w * me + w))
-    for lo, hi in parts:
-        dma("g", T.y[32 * lo:32 * hi, 0:a], T.ly0[lo:hi], "gy", full, [reg("ly0", lo, hi)], [])
-    for i, p in enumerate(("pb", "pa")):
+    dma("g", T.y[:, 0:4 * W0], T.zo[every], "gy", 16, [reg("zo", 0, 2)], [])
+    for i, p in enumerate(("pa", "pc")):
         z, nt = TURN[i][0], len(TURN[i][1])
         half = [(0, (nt + 1) // 2), ((nt + 1) // 2, nt)]
         for h, (lo, hi) in enumerate(half):
@@ -428,7 +459,9 @@ def rank_program(g, core, T, topo):
                 actv(o, q, act.Identity, 0.0, -1.0)
             else:
                 ts(o, q, -1.0, mult)
-        dma("y", T.y[:, z:z + 128 * nt], T.LF[:, z:z + 128 * nt], "y%d" % i, 16, [reg("LF", z, z + 128 * nt)], [])
+        for k, (lo, hi) in zip("ys", half) if i else (("y", (0, nt)),):
+            a, b = z + 128 * lo, z + 128 * hi
+            dma(k, T.y[:, a:b], T.LF[:, a:b], "y%d" % i, 32 if i else 16, [reg("LF", a, b)], [])
     for sem in total:
         if waited.get(sem, 0) < total[sem]:
             g.wait_ge(T.sem[sem], total[sem])

@@ -3,7 +3,7 @@ from concourse.mybir import AluOpType, ActivationFunctionType
 
 S = 1568
 HALF = 128.500244140625
-PAR = {"A": ((512, None), (640, "pa")), "AO": [(0, 0), (0, 1), (1, 0), (1, 1), (2, 0), (2, 1)], "B": (512, 256), "C": (512, 224), "D": (512, 224), "E": (384, 416), "T": (4, 2), "G": 1, "P": ((("v", 320, 480), 320, 480), (("s", 0, 224), 0, 160), (("v", 224, 320), 160, 320)), "BC": ((0, "v"), (1, "s"), (2, "v")), "M": {2: "sv", 3: "ss", 6: "ss"}, "FZ": 256, "AC": 416, "IL": 2, "AL": "pc", "NE": (1, 4)}
+PAR = {"A": ((512, None), (576, "pa")), "AO": "Y1 Y2 X2 k0a k0b x0a x0b - R0a R0b F0a F0b g1a g1b m1a m1b R1a R1b F1a F1b p2a p2b m2a m2b t2a t2b", "K": {2: 2, 3: 2, 6: 2}, "BO": "0a 0b 1a 1b 2a 2b ta tb", "TO": "0s3 0v0 1v0 0s4 0v1a 0v1b 0v2a 0s5a 0v2b 0s5b 1s4 1v1 e 1v2 1s5a 1s5b", "FV": 384, "CI": 1, "B": (512, 224), "C": (480, 192), "D": (512, 224), "E": (384, 416), "T": (4, 2), "G": 1, "P": ((("v", 320, 480), 320, 480), (("s", 0, 224), 0, 160), (("v", 224, 320), 160, 320)), "BC": ((0, "v"), (1, "s"), (2, "v")), "M": {2: "ss", 3: "ss", 6: "ss"}, "FZ": 256, "AC": 416, "IL": 2, "AL": "pc", "NE": (1, 4)}
 W0 = sum(PAR["E"]) // 4
 BANKS = [(p, a, a + 128) for p in ("pa", "pc", "pd", "pb") for a in (512, 0)]
 TURN = [(4 * W0, BANKS[0:PAR["T"][0]]), (S - 128 * PAR["T"][1], BANKS[PAR["T"][0]:sum(PAR["T"])])]
@@ -18,7 +18,7 @@ SCRATCH = {
     "IW": ("sbuf", [128, 128], "int32"), "IB": ("sbuf", [128, 128], "int32"), "JW": ("sbuf", [128, 128], "int32"),
     "JB": ("sbuf", [128, 128], "bfloat16"),
     "W": ("sbuf", [128, 256], "bfloat16"), "NI": ("sbuf", [128, 128], "bfloat16"), "WF": ("sbuf", [128, 128], "float32"),
-    "BK": ("sbuf", [128, 2048], "bfloat16"), "RB": ("sbuf", [128, 98], "bfloat16"), "K": ("sbuf", [128, 512], "float32"),
+    "BK": ("sbuf", [128, 2048], "bfloat16"), "RB": ("sbuf", [128, 98], "bfloat16"), "K": ("sbuf", [128, 640], "float32"),
     "N0": ("sbuf", [128, 2048], "bfloat16"), "N1": ("sbuf", [128, 2048], "float32"),
     "ON0": ("sbuf", [128, 4 * W0], "float16"), "WH": ("sbuf", [128, 128], "float16"),
     "Z0": ("sbuf", [128, 128 * PAR["T"][0]], "float16"), "Z1": ("sbuf", [128, 128 * PAR["T"][1]], "float16"),
@@ -209,6 +209,10 @@ def rank_program(g, core, T, topo):
             m = min(512, n - c)
             mm((pb, p0 + c, p0 + c + m), lhs, (rb, r0 + c, r0 + c + m), start, stop)
 
+    def first(p, lhs, buf, a, ns):
+        mm((p, 0, ns[0]), lhs, (buf, a, a + ns[0]), True, False)
+        mm((p, 512, 512 + ns[1]), lhs, (buf, a + ns[0], a + ns[0] + ns[1]), True, False)
+
     EYE, NEG, EYF, EYH = ("W", 0, 128), ("NI", 0, 128), ("WF", 0, 128), ("WH", 0, 128)
 
     out = slice(MID - me, MID - me + N)
@@ -277,31 +281,36 @@ def rank_program(g, core, T, topo):
             [reg("CPL", 294 * j, 294 * j + 294)])
 
     def wanted(s, win, lst, chunks, fw, between=None):
-        for a, n, k in chunks:
-            if k[0] != "K":
-                pick("s", ("X2_%d" % s, a, a + n), win, 2048, lst, 98 + a // 16)
-        both = S - PAR["AC"]
-        if both < S:
-            pick("s", ("VT_%d" % s, both, S), win, 2048, lst, both // 16)
-            mm(("pd", 0, S - both), EYE, ("VT_%d" % s, both, S), True, True)
-        between()
-        for i, (a, n, k) in enumerate(chunks):
-            ta, tp, fa, x2 = [("%s_%d" % (b, s), a, a + n) for b in ("TA", "TP", "FA", "X2")]
-            k, f = (k[0], k[1], k[1] + n), (fw, a, a + n)
-            if k[0] == "K":
+        for w in PAR["AO"].split():
+            if w == "-":
+                between()
+                if s == 0:
+                    copy("v", ("LST", 196, 226), ("E32", 196, 226))
+                continue
+            a0, n0, k = chunks[int(w[1])]
+            h = n0 // 64 * 32
+            lo, hi = {"": (0, n0), "a": (0, h), "b": (h, n0)}[w[2:]]
+            a, b = a0 + lo, a0 + hi
+            ta, tp, fa, x1, x2 = [("%s_%d" % (x, s), a, b) for x in ("TA", "TP", "FA", "VT", "X2")]
+            k, f = (k[0], k[1] + lo, k[1] + hi), (fw, a, b)
+            if w[0] == "k":
                 pickop(ta, win, 2048, lst, a // 16, k, mult)
+            elif w[0] == "x":
                 pickop(tp, win, 2048, lst, 98 + a // 16, ta, mult)
-            else:
-                b = min(a + n, max(a, both))
-                if a < b:
-                    pickop((ta[0], a, b), win, 2048, lst, a // 16, (x2[0], a, b), mult)
-                if b < a + n:
-                    tt((ta[0], b, a + n), ("pd", b - both, a + n - both), (x2[0], b, a + n), mult)
+            elif w[0] == "Y":
+                pick("s", x2, win, 2048, lst, 98 + a // 16)
+            elif w[0] == "X":
+                pick("s", x1, win, 2048, lst, a // 16)
+                mm(("pd", lo, hi), EYE, x1, True, True)
+            elif w[0] == "g":
+                pickop(ta, win, 2048, lst, a // 16, x2, mult)
+            elif w[0] == "p":
+                tt(ta, ("pd", lo, hi), x2, mult)
+            elif w[0] == "m":
                 tt(tp, k, ta, mult)
-            if s + i == 0:
-                copy("v", ("LST", 196, 226), ("E32", 196, 226))
-            if i < len(chunks) - 1:
+            elif w[0] == "R":
                 actv(fa, tp, act.Relu, 3.5, -1.0)
+            elif w[0] == "F":
                 actv(f, fa, act.Identity, 3.5 + HALF, -1.0)
             else:
                 ts(f, tp, 3.4, amin, HALF, add)
@@ -331,6 +340,10 @@ def rank_program(g, core, T, topo):
             copy("s", ("K", 0, KA), ("pb", 0, KA))
         if e == 1 and PAR["FZ"]:
             actv(("FB_%d" % s, 0, PAR["FZ"]), (win, 0, PAR["FZ"]), act.Identity, -129.0, 1.0)
+        if e in (1, 2):
+            a = PAR["FZ"] + PAR["FV"]
+            a, b = (PAR["FZ"], a) if e == 1 else (a, S - sum(PAR["C"]))
+            ts(("FB_%d" % s, a, b), ("FW_%d" % s, a, b), -129.0, add)
         for i, k in PAR["BC"]:
             a, b, p, p0 = pieces[i][1:]
             m = 2 - a // 160
@@ -349,26 +362,38 @@ def rank_program(g, core, T, topo):
             spread("pa", 0, KA, KL)
         spread("pc", 0, KL, S)
         wanted(s, NW, "LST", [(0, KA, ("K", 0)), (KA, KL - KA, ("pa", 0)), (KL, S - KL, ("pc", 0))], FW,
-               lambda: mmw("pb", 0, EN, NW, 0, A, True, False))
+               lambda: first("pb", EN, NW, 0, PAR["B"]))
         border(s, 1, FW, RXL)
 
         def scalar_part(p, buf, win, wn, lst, c0, signs, a, n0, n1, fin, *fn):
-            for j, sg in enumerate(signs):
-                last = j == len(signs) - 1
-                for b, n in ((0, n0), (n0, n1)) if last else ((0, n0 + n1),):
-                    pick("s", (buf, S * j + a + b, S * j + a + b + n), win, wn, lst, c0 + 98 * j + (a + b) // 16, *fn)
-                    mmw(p, b, sg, buf, S * j + a + b, n, False, last)
-            m = PAR["M"][len(signs)]
+            J = len(signs)
+            cut = J - PAR["K"][J]
+            halves = ((0, n0, 0), (n0, n1, 512))
+            for j, hs in [(j, halves) for j in range(cut)] + [(j, (h,)) for h in halves for j in range(cut, J)]:
+                b, n = hs[0][0], sum(h[1] for h in hs)
+                pick("s", (buf, S * j + a + b, S * j + a + b + n), win, wn, lst, c0 + 98 * j + (a + b) // 16, *fn)
+                for b, n, p0 in hs:
+                    mm((p, p0, p0 + n), signs[j], (buf, S * j + a + b, S * j + a + b + n), False, j == J - 1)
+            m = PAR["M"][J]
             fin(m[0], a, n0, (p, 0, n0))
-            fin(m[1], a + n0, n1, (p, n0, n0 + n1))
+            fin(m[1], a + n0, n1, (p, 512, 512 + n1))
         DB = nm("DB")
         C = S - sum(PAR["C"])
-        mmw("pa", 0, EYE, FW, C, S - C, True, False)
-        for c in range(3):
-            pickop((DB, A, S), FW, 2049, "CPL", 98 * c + A // 16, (NW if c == 0 else DB, A, S), sub if c == 0 else add)
-            if c == 0:
-                ts((nm("FB"), PAR["FZ"], C), (FW, PAR["FZ"], C), -129.0, add)
-        ts((UW, A, S), (DB, A, S), 3 * 129.0, le, 3.0, mult)
+        first("pa", EYE, FW, C, PAR["C"])
+        h = A + (S - A) // 64 * 32
+        z0 = PAR["FZ"] + PAR["FV"]
+        z1 = (z0 + C) // 2
+        part = {"": (A, S), "a": (A, h), "b": (h, S)}
+        for w in PAR["BO"].split():
+            if w[0] == "z":
+                a, b = {"": (z0, C), "a": (z0, z1), "b": (z1, C)}[w[1:]]
+                ts((nm("FB"), a, b), (FW, a, b), -129.0, add)
+            elif w[0] == "t":
+                a, b = part[w[1:]]
+                ts((UW, a, b), (DB, a, b), 3 * 129.0, le, 3.0, mult)
+            else:
+                c, (a, b) = int(w[0]), part[w[1:]]
+                pickop((DB, a, b), FW, 2049, "CPL", 98 * c + a // 16, (NW if c == 0 else DB, a, b), sub if c == 0 else add)
         scalar_part("pb", nm("DG"), FW, 2049, "CPL", 0, (NEG, NEG, NEG), 0, PAR["B"][0], PAR["B"][1],
                     lambda k, a, n, p: actv((UW, a, a + n), p, act.Relu, 3.0 + 9 * 129, 3.0) if k == "s" else
                     ts((UW, a, a + n), p, -3 * 129.0, AluOpType.is_ge, 3.0, mult))
@@ -376,9 +401,12 @@ def rank_program(g, core, T, topo):
         VT = nm("VT")
         e0, e1 = PAR["E"]
         if s == 0:
-            mmw("pb", 0, EN, NW, 0, sum(PAR["D"]), True, False)
-        pickop((VT, 0, C), UW, 2048, "LST", RE, (nm("FB"), 0, C), amin)
-        pickop((GW, 0, C), UW, 2048, "LST", RE + 98, (VT, 0, C), amin)
+            first("pb", EN, NW, 0, PAR["D"])
+        hs = ((0, C // 64 * 32), (C // 64 * 32, C)) if PAR["CI"] else ((0, C),)
+        for a, b in hs:
+            pickop((VT, a, b), UW, 2048, "LST", RE + a // 16, (nm("FB"), a, b), amin)
+        for a, b in hs:
+            pickop((GW, a, b), UW, 2048, "LST", RE + 98 + a // 16, (VT, a, b), amin)
         scalar_part("pa", nm("VG"), UW, 2048, "LST", RE, (NEG, NEG), C, PAR["C"][0], PAR["C"][1],
                     lambda k, a, n, p: actv((GW, a, a + n), p, act.Relu, -129.0, 1.0) if k == "s" else
                     ts((GW, a, a + n), p, -129.0, add, 0.0, AluOpType.max), act.Relu, 3.0, -1.0)
@@ -404,8 +432,11 @@ def rank_program(g, core, T, topo):
                 pick("s", (UG, S * j + a, S * j + a + n), GW, 2049, "CPL", 98 * j + a // 16)
                 mm(("pb", p0, p0 + n), signs[j], (UG, S * j + a, S * j + a + n), False, j == 5)
 
-            def turned(i, k, j):
+            def turned(i, k, j, h=""):
                 z, banks = TURN[i]
+                if h:
+                    m = len(banks) // 2
+                    z, banks = (z, banks[:m]) if h == "a" else (z + 128 * m, banks[m:])
                 n = 128 * len(banks)
                 if k == "s":
                     o = (UG, S * j + z, S * j + z + n)
@@ -430,11 +461,11 @@ def rank_program(g, core, T, topo):
             turned(1, "s", 3)
             vector_part(e0, e1, ("ON0", e0, e0 + e1))
             dma("y", T.zo[out], T.ON0[:], "o0", 16, [reg("ON0", 0, 4 * W0)], [reg("zo", 0, 1)])
-            for i, k, j in ((0, "s", 3), (0, "v", 0), (0, "s", 4), (0, "v", 1), (0, "v", 2), (0, "s", 5), (1, "s", 4), (1, "v", 0), (1, "v", 1)):
-                turned(i, k, j)
-            empty(0)
-            for k, j in (("v", 2), ("s", 5)):
-                turned(1, k, j)
+            for w in PAR["TO"].split():
+                if w == "e":
+                    empty(0)
+                else:
+                    turned(int(w[0]), w[1], int(w[2]), w[3:])
             empty(1)
 
     turn("zo", "ay0", 1)

from concourse.bass import DstId, RemoteDMATransfer
from concourse.mybir import AluOpType, ActivationFunctionType

S = 1568
HALF = 128.500244140625
PAR = {"A": ((512, None), (576, "pa")), "AO": "Y1 Y2 X2 k0a k0b x0a x0b - R0a R0b F0a F0b g1a g1b m1a m1b R1a R1b F1a F1b p2a p2b m2a m2b t2a t2b", "K": {2: 2, 3: 2, 6: 2}, "BO": "0a 0b 1a 1b 2a 2b ta tb", "TO": "0s3 0v0 1v0 0s4 0v1a 0v1b 0v2a 0s5a 0v2b 0s5b 1s4 1v1 e 1v2 1s5a 1s5b", "FV": 384, "CI": 1, "B": (512, 224), "C": (480, 192), "D": (512, 224), "E": (384, 416), "T": (4, 2), "G": 1, "P": ((("v", 320, 480), 320, 480), (("s", 0, 224), 0, 160), (("v", 224, 320), 160, 320)), "BC": ((0, "v"), (1, "s"), (2, "v")), "M": {2: "ss", 3: "ss", 6: "ss"}, "FZ": 256, "AC": 416, "IL": 2, "AL": "pc", "NE": (1, 4)}
W0 = sum(PAR["E"]) // 4
BANKS = [(p, a, a + 128) for p in ("pa", "pc", "pd", "pb") for a in (512, 0)]
TURN = [(4 * W0, BANKS[0:PAR["T"][0]]), (S - 128 * PAR["T"][1], BANKS[PAR["T"][0]:sum(PAR["T"])])]
MID, SLOTS = 12, 25

SCRATCH = {
    "ze": ("dram", [SLOTS, 128, 64], "int32"), "zr": ("dram", [SLOTS, 128, 32], "int32"),
    "zl": ("dram", [SLOTS, 128, 147], "uint16"),
    "X32": ("sbuf", [128, S], "int32"), "XO": ("sbuf", [128, S], "int32"), "X16": ("sbuf", [128, S], "bfloat16"),
    "XL": ("sbuf", [128, S], "bfloat16"),
    "E32": ("sbuf", [128, 354], "int32"), "LST": ("sbuf", [128, 256], "uint16"), "CPL": ("sbuf", [128, 588], "uint16"),
    "IW": ("sbuf", [128, 128], "int32"), "IB": ("sbuf", [128, 128], "int32"), "JW": ("sbuf", [128, 128], "int32"),
    "JB": ("sbuf", [128, 128], "bfloat16"),
    "W": ("sbuf", [128, 256], "bfloat16"), "NI": ("sbuf", [128, 128], "bfloat16"), "WF": ("sbuf", [128, 128], "float32"),
    "BK": ("sbuf", [128, 2048], "bfloat16"), "RB": ("sbuf", [128, 98], "bfloat16"), "K": ("sbuf", [128, 640], "float32"),
    "N0": ("sbuf", [128, 2048], "bfloat16"), "N1": ("sbuf", [128, 2048], "float32"),
    "ON0": ("sbuf", [128, 4 * W0], "float16"), "WH": ("sbuf", [128, 128], "float16"),
    "Z0": ("sbuf", [128, 128 * PAR["T"][0]], "float16"), "Z1": ("sbuf", [128, 128 * PAR["T"][1]], "float16"),
    "L0": ("sbuf", [128, 128 * PAR["T"][0]], "float16"), "L1": ("sbuf", [128, 128 * PAR["T"][1]], "float16"),
    "LF": ("sbuf", [128, S], "float32"), "UH": ("sbuf", [128, S], "float16"),
    "pa": ("psum", [128, 1024], "float32"), "pb": ("psum", [128, 1024], "float32"),
    "pc": ("psum", [128, 1024], "float32"), "pd": ("psum", [128, 1024], "float32"),
    "zo": ("dram", [SLOTS, 128, W0], "float16"),
}
for _s in range(2):
    for _n, _w, _d in (("SE0", 480, "bfloat16"), ("SE1", 480, "bfloat16"), ("SE2", 480, "bfloat16"), ("SE3", 480, "bfloat16"),
                       ("X2", S, "bfloat16"),
                       ("TA", S, "float32"), ("TP", S, "float32"), ("FA", S, "float32"), ("FB", S, "bfloat16"),
                       ("FW", 2064, "bfloat16"), ("UW", 2048, "bfloat16"), ("GW", 2064, "bfloat16"),
                       ("DG", 3 * S, "bfloat16"), ("DB", S, "float16"), ("VT", S, "bfloat16"), ("VG", 2 * S, "bfloat16"),
                       ("UG", 6 * S, "bfloat16"), ("UA", S, "float32")):
        SCRATCH["%s_%d" % (_n, _s)] = ("sbuf", [128, _w], _d)

SEMAPHORES = (["cv", "cs", "ct", "cg", "rl", "se", "sl", "gy", "ER", "EL", "EX", "CC", "CP", "o0",
               "ay0", "az0", "az1", "y0", "y1", "ae", "al", "ar", "sr", "ES"] + ["%s%d" % (a, r) for a in ("ax", "gx") for r in range(4)])


def masks(src, cores, topo, k):
    others = [c for c in cores if c != src]
    eng = dict((c, list(topo.engines(src, c))) for c in others)
    few = min(len(eng[c]) for c in others)
    far = [c for c in others if len(eng[c]) == few]
    share = len(eng[far[0]]) // len(far)
    share = 1 << (share.bit_length() - 1)
    out = {}
    for i, c in enumerate(far):
        out[c] = eng[c][i * share:(i + 1) * share][0:k]
    for c in others:
        if c not in out:
            out[c] = [e for e in eng[c] if e not in eng[far[0]]][0:2 * k:2]
    return out


def runs(ranks):
    out = []
    for r in sorted(ranks):
        if out and out[-1][1] == r:
            out[-1] = (out[-1][0], r + 1)
        else:
            out.append((r, r + 1))
    return out


def rank_program(g, core, T, topo):
    me = T.rank_of(core)
    if me is None:
        return
    add, sub, mult, amin = AluOpType.add, AluOpType.subtract, AluOpType.mult, AluOpType.min
    eq, le = AluOpType.is_equal, AluOpType.is_le
    act = ActivationFunctionType
    cores = list(T.cores)
    N = len(cores)
    others = [r for r in range(N) if r != me]
    near = [r for r in others if cores[r] in topo.cores_of(core)]
    order = near + [r for r in others if r not in near]
    engs = [masks(core, cores, topo, k) for k in PAR["NE"]]
    incs = [dict((r, len(masks(cores[r], cores, topo, k)[core])) for r in others) for k in PAR["NE"]]

    queue = {"v": g.vector, "s": g.scalar, "t": g.tensor, "g": g, "y": g.sync}
    total, waited, hist = {}, {}, {}
    know = dict((k, {}) for k in queue)

    def wait(k, toks):
        best = {}
        for sem, val, clock in toks:
            if know[k].get(sem, 0) < val and (sem not in best or best[sem][1] < val):
                best[sem] = (sem, val, clock)
        todo = [t for t in best.values() if not any(u[0] != t[0] and u[2].get(t[0], 0) >= t[1] for u in best.values())]
        for sem, val, clock in todo:
            queue[k].wait_ge(T.sem[sem], val)
            waited[sem] = max(waited.get(sem, 0), val)
            for s, v in list(clock.items()) + [(sem, val)]:
                know[k][s] = max(know[k].get(s, 0), v)

    def hazards(k, rd, wr):
        toks = []
        for kind, regs in ((0, rd), (1, wr)):
            for b, lo, hi, p0, p1 in regs:
                bank = b[0] == "p"
                for lo2, hi2, q0, q1, w2, tok, k2 in hist.get(b, []):
                    if bank and k2 != k:
                        hit = lo // 512 <= (hi2 - 1) // 512 and lo2 // 512 <= (hi - 1) // 512
                    elif bank:
                        hit = False
                    else:
                        hit = lo < hi2 and lo2 < hi and p0 < q1 and q0 < p1 and (kind or w2)
                    if hit:
                        toks.append(tok)
        return toks

    def note(k, rd, wr, tok):
        for w, regs in ((0, rd), (1, wr)):
            for b, lo, hi, p0, p1 in regs:
                hist.setdefault(b, []).append((lo, hi, p0, p1, w, tok, k))

    def reg(b, lo, hi, p0=0, p1=128):
        return (b, lo, hi, p0, p1)

    def op(k, rd, wr, call):
        wait(k, hazards(k, rd, wr))
        sem = "c" + k
        total[sem] = total.get(sem, 0) + 1
        clock = dict(know[k])
        clock[sem] = total[sem]
        note(k, rd, wr, (sem, total[sem], clock))
        call().then_inc(T.sem[sem], 1)

    def dma(k, out, in_, sem, full, rd, wr):
        wait(k, hazards(k, rd, wr))
        total[sem] = total.get(sem, 0) + 16
        note(k, rd, wr, (sem, full, dict(know[k]) if full == 16 else {}))
        queue[k].dma_start(out, in_).then_inc(T.sem[sem], 16)

    def send(src, dst, sems, rd, wide, to=order):
        wait("g", hazards("g", rd, []))
        eng = engs[wide]
        trs = []
        for r in to:
            rid, pid = topo.addr(cores[r], core)
            bits = [1 << e for e in eng[cores[r]]]
            for m, a, b in zip(bits, src, dst) if isinstance(src, list) else ((sum(bits), src, dst),):
                trs.append(RemoteDMATransfer(dst_ids=[DstId(rid=rid, pnc=pid)], dma_engine_mask=m, remote_sem=T.sem[sems],
                                             src=a(r), dst=b(r)))
            total["rl"] = total.get("rl", 0) + len(bits)
        g.remote_dma_fused(trs, local_sem=T.sem["rl"])

    def arrives(sem, regs, srcs, wide=0):
        n = sum(incs[wide][r] for r in srcs)
        total[sem] = total.get(sem, 0) + n
        note("r", [], regs, (sem, n, {}))

    def ap(x):
        return T[x[0]][:, x[1]:x[2]]

    def ind(win, wn, lst, c0, n):
        return T[win][:, 0:wn].indirect(T[lst][:, c0:c0 + n // 16])

    def pick(k, out, win, wn, lst, c0, func=None, bias=0.0, scale=1.0):
        n = out[2] - out[1]
        rd = [reg(win, 0, wn), reg(lst, c0, c0 + n // 16)]
        if k == "v":
            op("v", rd, [reg(*out)], lambda: g.vector.tensor_copy(out=ap(out), in_=ind(win, wn, lst, c0, n)))
        elif func is None:
            op("s", rd, [reg(*out)], lambda: g.scalar.activation(out=ap(out), in_=ind(win, wn, lst, c0, n), func=act.Copy))
        else:
            op("s", rd, [reg(*out)], lambda: g.scalar.activation(out=ap(out), in_=ind(win, wn, lst, c0, n), func=func,
                                                                 bias=bias, scale=scale))

    def pickop(out, win, wn, lst, c0, other, o):
        n = out[2] - out[1]
        op("v", [reg(win, 0, wn), reg(lst, c0, c0 + n // 16), reg(*other)], [reg(*out)],
           lambda: g.vector.tensor_tensor(out=ap(out), in0=ind(win, wn, lst, c0, n), in1=ap(other), op=o))

    def tt(out, a, b, o):
        op("v", [reg(*a), reg(*b)], [reg(*out)], lambda: g.vector.tensor_tensor(out=ap(out), in0=ap(a), in1=ap(b), op=o))

    def ts(out, a, s1, o1, s2=None, o2=None):
        if o2 is None:
            f = lambda: g.vector.tensor_scalar(out=ap(out), in0=ap(a), scalar1=s1, scalar2=None, op0=o1)
        else:
            f = lambda: g.vector.tensor_scalar(out=ap(out), in0=ap(a), scalar1=s1, scalar2=s2, op0=o1, op1=o2)
        op("v", [reg(*a)], [reg(*out)], f)

    def actv(out, a, func, bias=0.0, scale=1.0):
        if func == act.Copy:
            f = lambda: g.scalar.activation(out=ap(out), in_=ap(a), func=func)
        else:
            f = lambda: g.scalar.activation(out=ap(out), in_=ap(a), func=func, bias=bias, scale=scale)
        op("s", [reg(*a)], [reg(*out)], f)

    def copy(k, out, a):
        if k == "v":
            op("v", [reg(*a)], [reg(*out)], lambda: g.vector.tensor_copy(out=ap(out), in_=ap(a)))
        else:
            actv(out, a, act.Copy)

    def mm(out, lhs, rhs, start, stop):
        op("t", [reg(*lhs), reg(*rhs)], [reg(*out)],
           lambda: g.tensor.matmul(out=ap(out), lhsT=ap(lhs), rhs=ap(rhs), start=start, stop=stop))

    def mmw(pb, p0, lhs, rb, r0, n, start, stop):
        for c in range(0, n, 512):
            m = min(512, n - c)
            mm((pb, p0 + c, p0 + c + m), lhs, (rb, r0 + c, r0 + c + m), start, stop)

    def first(p, lhs, buf, a, ns):
        mm((p, 0, ns[0]), lhs, (buf, a, a + ns[0]), True, False)
        mm((p, 512, 512 + ns[1]), lhs, (buf, a + ns[0], a + ns[0] + ns[1]), True, False)

    EYE, NEG, EYF, EYH = ("W", 0, 128), ("NI", 0, 128), ("WF", 0, 128), ("WH", 0, 128)

    out = slice(MID - me, MID - me + N)

    def inn(lo, hi):
        return slice(MID + 4 * (lo - me), MID + 4 * (hi - 1 - me) + 1, 4)

    def turn(z, sem, wide=0):
        send(lambda r: T[z][MID + r - me], lambda r: T[z][MID + 4 * (me - r)], sem, [reg(z, 0, 1)], wide)
    op("g", [], [reg("IB", 0, 128)], lambda: g.iota(T.IB[:], [[-16, 8], [0, 16]], 0, 1))
    op("g", [], [reg("IW", 0, 128)], lambda: g.iota(T.IW[:], [[-1, 128]], 0, 1))
    for b in ("FW_0", "GW_0", "FW_1", "GW_1"):
        op("v", [], [reg(b, 2048, 2064)], lambda: g.vector.memset(T[b][:, 2048:2064], 129.0 if b[0] == "F" else 0.0))
    copy("v", ("JB", 0, 128), ("IB", 0, 128))
    for c in range(16):
        ts(("BK", 128 * c, 128 * c + 128), ("JB", 0, 128), c, eq, 1.0 / 1024, mult)
    for k, a, b, t in (("y", 0, 98, T.rate), ("s", 98, 128, T.spsend)):
        dma(k, T.zr[out, a:b, :], t[:], "sr", 32, [], [reg("zr", 0, 1, a, b)])
    far = [r for r in others if r not in near]
    for r in far + near:
        a, b = 392 * r, 392 * r + 392
        for j in range(4):
            dma("ys"[j % 2], T.X32[32 * j:32 * j + 32, a:b], T.x[32 * r:32 * r + 32, 392 * j:392 * j + 392], "gx%d" % r, 64, [],
                [reg("X32", a, b, 32 * j, 32 * j + 32)])
        copy("v", ("X16", a, b), ("X32", a, b))
    mine = slice(32 * me, 32 * me + 32)
    dma("y", T.XO[mine, :], T.x[mine, :], "gx%d" % me, 16, [], [reg("XO", 0, S)])
    op("v", [reg("XO", 0, S)], [reg("N0", 0, S, 32 * me, 32 * me + 32)],
       lambda: g.vector.tensor_copy(out=T.N0[mine, 0:S], in_=T.XO[mine, :]))
    for k, a, b, t in (("y", 0, 98, T.reac), ("s", 98, 113, T.rxsend), ("s", 113, 128, T.rxsend)):
        dma(k, T.ze[out, a:b, :], t[:], "se", 48, [], [reg("ze", 0, 1, a, b)])
    turn("zr", "ar")
    arrives("ar", [reg("zr", 1, 2)], others)

    def spread(p, p0, a, b, rb="RB"):
        while a < b:
            c = a // 98
            n = min(b - a, 98 * (c + 1) - a, 512 - p0 % 512)
            mm((p, p0, p0 + n), ("BK", 128 * c, 128 * c + 128), (rb, a - 98 * c, a - 98 * c + n), True, True)
            a, p0 = a + n, p0 + n
    for to in (far, near):
        send(lambda r: T.X16[:, 392 * r:392 * r + 392], lambda r: T.XL[:, 392 * me:392 * me + 392], "ax%d" % me,
             [reg("X16", 392 * r, 392 * r + 392) for r in to], 1, to)
    for r in others:
        arrives("ax%d" % r, [reg("XL", 392 * r, 392 * r + 392)], [r], 1)
    turn("ze", "ae", 1)
    arrives("ae", [reg("ze", 1, 2)], others, 1)
    for j, t in enumerate((T.cons, T.prod)):
        dma("g", T.zl[out, 64 * j:64 * j + 64, :], t[:], "sl", 32, [], [reg("zl", 0, 1, j, j + 1)])
    turn("zl", "al", 1)
    arrives("al", [reg("zl", 1, 2)], others, 1)
    ts(("W", 0, 128), ("IW", 0, 128), 0, eq)
    ts(("W", 128, 256), ("IW", 0, 128), 0, eq)
    ts(("NI", 0, 128), ("IW", 0, 128), 0, eq, -1, mult)
    ts(("WF", 0, 128), ("IW", 0, 128), 0, eq)
    ts(("WH", 0, 128), ("IW", 0, 128), 0, eq)

    RE, SP, RXL = 0, 226, 196
    every = inn(0, N)
    dma("y", T.E32[:, 256:354], T.zr[every, 0:98, :], "ER", 16, [reg("zr", 0, 2)], [reg("E32", 256, 354)])
    dma("s", T.E32[:, 226:256], T.zr[every, 98:128, :], "ES", 16, [reg("zr", 0, 2)], [reg("E32", 226, 256)])
    for sem, a, b, c, d in (("EL", 0, 98, 0, 196), ("EX", 98, 113, 196, 226)):
        dma("y", T.E32[:, c:d], T.ze[every, a:b, :], sem, 16, [reg("ze", 0, 2)], [reg("E32", c, d)])
    for j, sem in enumerate(("CC", "CP")):
        dma("y", T.CPL[:, 294 * j:294 * j + 294], T.zl[every, 64 * j:64 * j + 64, :], sem, 16, [reg("zl", 0, 2)],
            [reg("CPL", 294 * j, 294 * j + 294)])

    def wanted(s, win, lst, chunks, fw, between=None):
        for w in PAR["AO"].split():
            if w == "-":
                between()
                if s == 0:
                    copy("v", ("LST", 196, 226), ("E32", 196, 226))
                continue
            a0, n0, k = chunks[int(w[1])]
            h = n0 // 64 * 32
            lo, hi = {"": (0, n0), "a": (0, h), "b": (h, n0)}[w[2:]]
            a, b = a0 + lo, a0 + hi
            ta, tp, fa, x1, x2 = [("%s_%d" % (x, s), a, b) for x in ("TA", "TP", "FA", "VT", "X2")]
            k, f = (k[0], k[1] + lo, k[1] + hi), (fw, a, b)
            if w[0] == "k":
                pickop(ta, win, 2048, lst, a // 16, k, mult)
            elif w[0] == "x":
                pickop(tp, win, 2048, lst, 98 + a // 16, ta, mult)
            elif w[0] == "Y":
                pick("s", x2, win, 2048, lst, 98 + a // 16)
            elif w[0] == "X":
                pick("s", x1, win, 2048, lst, a // 16)
                mm(("pd", lo, hi), EYE, x1, True, True)
            elif w[0] == "g":
                pickop(ta, win, 2048, lst, a // 16, x2, mult)
            elif w[0] == "p":
                tt(ta, ("pd", lo, hi), x2, mult)
            elif w[0] == "m":
                tt(tp, k, ta, mult)
            elif w[0] == "R":
                actv(fa, tp, act.Relu, 3.5, -1.0)
            elif w[0] == "F":
                actv(f, fa, act.Identity, 3.5 + HALF, -1.0)
            else:
                ts(f, tp, 3.4, amin, HALF, add)

    def place(r, ks):
        for j, k in enumerate(ks):
            o, i = T.N0[32 * r:32 * r + 32, 392 * j:392 * j + 392], T.XL[32 * j:32 * j + 32, 392 * r:392 * r + 392]
            op(k, [reg("XL", 392 * r, 392 * r + 392)], [reg("N0", 392 * j, 392 * j + 392, 32 * r, 32 * r + 32)],
               lambda: g.vector.tensor_copy(out=o, in_=i) if k == "v" else g.scalar.activation(out=o, in_=i, func=act.Copy))
    for r, ks in zip(near + far, ("vvvs", "vvss")):
        place(r, ks)
    copy("v", ("RB", 0, 98), ("E32", 256, 354))
    KA, KL = PAR["A"][0][0], sum(n for n, p in PAR["A"])
    spread("pb", 0, 0, KA)
    place(far[-1], "vvvs")
    copy("v", ("LST", 226, 256), ("E32", 226, 256))

    def border(s, e, win, c0):
        se = "SE%d_%d" % (e, s)
        pieces = [x + y for x, y in zip(PAR["P"], (("pc", 0), ("pc", 512), ("pd", 0), ("pd", 512)))]
        for k, a, b, p, p0 in pieces:
            m = 2 - a // 160
            if k:
                pick(k[0], (se, k[1], k[2]), win, S, "LST", c0 + k[1] // 16)
            mm((p, p0, p0 + b - a), ("W", 32 * (1 + m), 32 * (1 + m) + 128), (se, a, b), True, True)
        if s + e == 0:
            copy("s", ("K", 0, KA), ("pb", 0, KA))
        if e == 1 and PAR["FZ"]:
            actv(("FB_%d" % s, 0, PAR["FZ"]), (win, 0, PAR["FZ"]), act.Identity, -129.0, 1.0)
        if e in (1, 2):
            a = PAR["FZ"] + PAR["FV"]
            a, b = (PAR["FZ"], a) if e == 1 else (a, S - sum(PAR["C"]))
            ts(("FB_%d" % s, a, b), ("FW_%d" % s, a, b), -129.0, add)
        for i, k in PAR["BC"]:
            a, b, p, p0 = pieces[i][1:]
            m = 2 - a // 160
            c = S + 160 * m + a % 160
            copy(k, (win, c, c + b - a), (p, p0, p0 + b - a))

    for s in range(2):
        def nm(b):
            return "%s_%d" % (b, s)
        NW, FW, UW, GW = "N%d" % s, nm("FW"), nm("UW"), nm("GW")
        EN = EYF if s else EYE
        border(s, 0, NW, SP)
        A = sum(PAR["B"])
        if s == 0:
            copy("v", ("LST", 0, 196), ("E32", 0, 196))
            spread("pa", 0, KA, KL)
        spread("pc", 0, KL, S)
        wanted(s, NW, "LST", [(0, KA, ("K", 0)), (KA, KL - KA, ("pa", 0)), (KL, S - KL, ("pc", 0))], FW,
               lambda: first("pb", EN, NW, 0, PAR["B"]))
        border(s, 1, FW, RXL)

        def scalar_part(p, buf, win, wn, lst, c0, signs, a, n0, n1, fin, *fn):
            J = len(signs)
            cut = J - PAR["K"][J]
            halves = ((0, n0, 0), (n0, n1, 512))
            for j, hs in [(j, halves) for j in range(cut)] + [(j, (h,)) for h in halves for j in range(cut, J)]:
                b, n = hs[0][0], sum(h[1] for h in hs)
                pick("s", (buf, S * j + a + b, S * j + a + b + n), win, wn, lst, c0 + 98 * j + (a + b) // 16, *fn)
                for b, n, p0 in hs:
                    mm((p, p0, p0 + n), signs[j], (buf, S * j + a + b, S * j + a + b + n), False, j == J - 1)
            m = PAR["M"][J]
            fin(m[0], a, n0, (p, 0, n0))
            fin(m[1], a + n0, n1, (p, 512, 512 + n1))
        DB = nm("DB")
        C = S - sum(PAR["C"])
        first("pa", EYE, FW, C, PAR["C"])
        h = A + (S - A) // 64 * 32
        z0 = PAR["FZ"] + PAR["FV"]
        z1 = (z0 + C) // 2
        part = {"": (A, S), "a": (A, h), "b": (h, S)}
        for w in PAR["BO"].split():
            if w[0] == "z":
                a, b = {"": (z0, C), "a": (z0, z1), "b": (z1, C)}[w[1:]]
                ts((nm("FB"), a, b), (FW, a, b), -129.0, add)
            elif w[0] == "t":
                a, b = part[w[1:]]
                ts((UW, a, b), (DB, a, b), 3 * 129.0, le, 3.0, mult)
            else:
                c, (a, b) = int(w[0]), part[w[1:]]
                pickop((DB, a, b), FW, 2049, "CPL", 98 * c + a // 16, (NW if c == 0 else DB, a, b), sub if c == 0 else add)
        scalar_part("pb", nm("DG"), FW, 2049, "CPL", 0, (NEG, NEG, NEG), 0, PAR["B"][0], PAR["B"][1],
                    lambda k, a, n, p: actv((UW, a, a + n), p, act.Relu, 3.0 + 9 * 129, 3.0) if k == "s" else
                    ts((UW, a, a + n), p, -3 * 129.0, AluOpType.is_ge, 3.0, mult))
        border(s, 2, UW, SP)
        VT = nm("VT")
        e0, e1 = PAR["E"]
        if s == 0:
            first("pb", EN, NW, 0, PAR["D"])
        hs = ((0, C // 64 * 32), (C // 64 * 32, C)) if PAR["CI"] else ((0, C),)
        for a, b in hs:
            pickop((VT, a, b), UW, 2048, "LST", RE + a // 16, (nm("FB"), a, b), amin)
        for a, b in hs:
            pickop((GW, a, b), UW, 2048, "LST", RE + 98 + a // 16, (VT, a, b), amin)
        scalar_part("pa", nm("VG"), UW, 2048, "LST", RE, (NEG, NEG), C, PAR["C"][0], PAR["C"][1],
                    lambda k, a, n, p: actv((GW, a, a + n), p, act.Relu, -129.0, 1.0) if k == "s" else
                    ts((GW, a, a + n), p, -129.0, add, 0.0, AluOpType.max), act.Relu, 3.0, -1.0)
        border(s, 3, GW, RXL)
        UA, UG = nm("UA"), nm("UG")
        signs = (NEG, NEG, NEG, EYE, EYE, EYE)

        def vector_part(a, n, o):
            h = n // 64 * 32 if PAR["IL"] > s else n
            for j in range(6):
                for b, c in ((0, h), (h, n)) if h < n else ((0, n),):
                    acc = (UA, a + b, a + c)
                    pickop((o[0], o[1] + b, o[1] + c) if j == 5 else acc, GW, 2049, "CPL", 98 * j + (a + b) // 16,
                           (NW, a + b, a + c) if j == 0 else acc, sub if j in (0, 3) else add)
        if s == 0:
            spread("pa", 0, KA, KL)
            a = sum(PAR["D"])
            vector_part(a, S - a, ("N1", a, S))
            scalar_part("pb", UG, GW, 2049, "CPL", 0, signs, 0, PAR["D"][0], PAR["D"][1],
                        lambda k, a, n, p: copy(k, ("N1", a, a + n), p))
        else:
            def us(a, n, j, p0):
                pick("s", (UG, S * j + a, S * j + a + n), GW, 2049, "CPL", 98 * j + a // 16)
                mm(("pb", p0, p0 + n), signs[j], (UG, S * j + a, S * j + a + n), False, j == 5)

            def turned(i, k, j, h=""):
                z, banks = TURN[i]
                if h:
                    m = len(banks) // 2
                    z, banks = (z, banks[:m]) if h == "a" else (z + 128 * m, banks[m:])
                n = 128 * len(banks)
                if k == "s":
                    o = (UG, S * j + z, S * j + z + n)
                    pick("s", o, GW, 2049, "CPL", 98 * j + z // 16)
                else:
                    o = ("UH" if j == 2 else UA, z, z + n)
                    pickop(o, GW, 2049, "CPL", 98 * j + z // 16, (UA if j else NW, z, z + n), add if j else sub)
                if (i, j) == (1, 3):
                    copy("s", ("ON0", 0, e0), ("pb", 0, e0))
                for t, p in enumerate(banks if j >= 2 else []):
                    mm(p, (o[0], o[1] + 128 * t, o[1] + 128 * t + 128), NEG if j > 2 else EYH, j == 3, j == 5)

            def empty(i):
                nt = len(TURN[i][1])
                for t, p in enumerate(TURN[i][1]):
                    o = T["Z%d" % i][:, t::nt]
                    op("vs"[t % 2], [reg(*p)], [reg("Z%d" % i, 0, 128 * nt, t, t + 1)],
                       lambda: g.scalar.activation(out=o, in_=ap(p), func=act.Copy) if t % 2 else g.vector.tensor_copy(out=o, in_=ap(p)))
            mm(("pb", 0, e0), EN, (NW, 0, e0), True, False)
            for j in range(6):
                us(0, e0, j, 0)
            turned(1, "s", 3)
            vector_part(e0, e1, ("ON0", e0, e0 + e1))
            dma("y", T.zo[out], T.ON0[:], "o0", 16, [reg("ON0", 0, 4 * W0)], [reg("zo", 0, 1)])
            for w in PAR["TO"].split():
                if w == "e":
                    empty(0)
                else:
                    turned(int(w[0]), w[1], int(w[2]), w[3:])
            empty(1)

    turn("zo", "ay0", 1)
    arrives("ay0", [reg("zo", 1, 2)], others, 1)
    for i in range(2):
        z, l, w = "Z%d" % i, "L%d" % i, 32 * len(TURN[i][1])
        send(lambda r: T[z][:, w * r:w * r + w], lambda r: T[l][:, w * me:w * me + w], "az%d" % i, [reg(z, 0, 4 * w)], 1)
        arrives("az%d" % i, [reg(l, w * r, w * r + w) for r in others], others, 1)
        copy("v", (l, w * me, w * me + w), (z, w * me, w * me + w))
    dma("g", T.y[:, 0:4 * W0], T.zo[every], "gy", 16, [reg("zo", 0, 2)], [])
    for i, p in enumerate(("pa", "pc")):
        z, nt = TURN[i][0], len(TURN[i][1])
        half = [(0, (nt + 1) // 2), ((nt + 1) // 2, nt)]
        for h, (lo, hi) in enumerate(half):
            for t in range(lo, hi):
                o = (p, 512 * h + 128 * (t - lo), 512 * h + 128 * (t - lo) + 128)
                op("t", [reg("L%d" % i, 0, 128 * nt), reg(*EYH)], [reg(*o)],
                   lambda: g.tensor.matmul(out=ap(o), lhsT=T["L%d" % i][:, t::nt], rhs=ap(EYH), start=True, stop=True))
        for h, (lo, hi) in enumerate(half):
            o, q = ("LF", z + 128 * lo, z + 128 * hi), (p, 512 * h, 512 * h + 128 * (hi - lo))
            if h:
                actv(o, q, act.Identity, 0.0, -1.0)
            else:
                ts(o, q, -1.0, mult)
        for k, (lo, hi) in zip("ys", half) if i else (("y", (0, nt)),):
            a, b = z + 128 * lo, z + 128 * hi
            dma(k, T.y[:, a:b], T.LF[:, a:b], "y%d" % i, 32 if i else 16, [reg("LF", a, b)], [])
    for sem in total:
        if waited.get(sem, 0) < total[sem]:
            g.wait_ge(T.sem[sem], total[sem])
